import numpy as np
import ml_dtypes


def mxq(x, axis, fmt="e4m3"):
    dtype, down = {"e4m3": (ml_dtypes.float8_e4m3fn, 7), "e5m2": (ml_dtypes.float8_e5m2, 14)}[fmt]
    v = np.moveaxis(np.asarray(x, np.float32).astype(ml_dtypes.bfloat16).astype(np.float64), axis, -1)
    blocks = v.reshape(v.shape[:-1] + (-1, 32))
    amax = np.abs(blocks).max(-1, keepdims=True)
    byte = np.maximum(np.where(amax > 0, np.frexp(amax)[1] - 1 + 127, 0) - down, 1)
    scale = np.exp2(byte - 127.0)
    codes = (blocks / scale).astype(np.float32).astype(dtype).astype(np.float64)
    return np.moveaxis((codes * scale).reshape(v.shape), -1, axis)


WIDE = False


def mx_kscale(k):
    if not WIDE:
        return np.ones(k)
    levels = np.array([24, -24, 12, -12, 0])
    if k % 512:
        return np.exp2(np.random.permutation(np.resize(levels, k // 32))).repeat(32)
    a = np.empty((k // 512, 16))
    for p in range(k // 512):
        a[p, :8] = np.random.permutation(np.resize(levels, 8))
        for g in range(8):
            far = levels[np.abs(levels - a[p, g]) >= 10]
            a[p, g + 8] = far[np.random.randint(len(far))]
    return np.exp2(a.ravel()).repeat(32)


def f64(x):
    return np.asarray(x).astype(np.float64)


def striped(idx):
    return np.tile(idx.reshape(-1, 16).T, (8, 1)).astype(np.uint16)


def unstriped(offs):
    return offs[:16].T.reshape(-1).astype(np.int64)


E2M1 = np.array([0.0, 0.5, 1.0, 1.5, 2.0, 3.0, 4.0, 6.0, -0.0, -0.5, -1.0, -1.5, -2.0, -3.0, -4.0, -6.0])


def pack_weight(w, fmt):
    k, n = w.shape
    w = f64(np.asarray(w, np.float32).astype(ml_dtypes.bfloat16)).reshape(k // 32, 32, n)
    amax = np.abs(w).max(1)
    if fmt == "e4m3":
        byte = np.frexp(amax)[1] - 1 + 127 - 7
    else:
        mant, ex = np.frexp(amax / 6.0)
        byte = np.where(mant > 0.5, ex, ex - 1) + 127
    byte = np.clip(np.where(amax > 0, byte, 1), 1, 254)
    scaled = (w * np.exp2(127.0 - byte)[:, None, :]).reshape(k, n).astype(np.float32)
    by_word = np.ascontiguousarray(scaled.reshape(k // 512, 128, 4, n).transpose(0, 1, 3, 2))
    if fmt == "e4m3":
        words = by_word.astype(ml_dtypes.float8_e4m3fn).view(np.uint8)
    else:
        c = by_word.astype(ml_dtypes.float4_e2m1fn).view(np.uint8) & 0xF
        words = (c[..., 0::2] | (c[..., 1::2] << 4)).reshape(k // 512, 128, 2 * n)
    return np.ascontiguousarray(words), np.ascontiguousarray(byte.astype(np.uint8).reshape(k // 512, 16, n))


def unpack_weight(words, scales, fmt):
    g, _, n = scales.shape
    words = np.ascontiguousarray(words).reshape(g, 128, n, -1)
    if fmt == "e4m3":
        vals = words.view(ml_dtypes.float8_e4m3fn).astype(np.float64)
    else:
        nib = np.empty((g, 128, n, 4), np.uint8)
        nib[..., 0::2] = words & 0xF
        nib[..., 1::2] = words >> 4
        vals = E2M1[nib]
    vals = vals * np.repeat(np.exp2(scales.astype(np.float64) - 127.0), 8, axis=1)[..., None]
    return vals.transpose(0, 1, 3, 2).reshape(g * 512, n)


K, L, R, N, T, J = 512, 512, 512, 512, 1024, 512


def setup_inputs():
    n = np.random.standard_normal
    s = mx_kscale(K)[:, None]
    s2 = mx_kscale(L)[:, None]
    u = mx_kscale(R)[:, None]
    p_tab = pack_weight(n((K, T)) * s, "e4m3")
    p_tab2 = pack_weight(n((L, T)) * s2, "e4m3")
    p_wb = pack_weight(n((L, R)) / np.sqrt(L) / s2 * u.T, "e2m1")
    return {
        "tab_words": p_tab[0],
        "tab_scales": p_tab[1],
        "tab2_words": p_tab2[0],
        "tab2_scales": p_tab2[1],
        "wa": (n((K, R)) / np.sqrt(K) / s * u.T).astype(np.float32),
        "wb_words": p_wb[0],
        "wb_scales": p_wb[1],
        "en": (n((R, N)) / np.sqrt(R) / u).astype(np.float32),
        "offs": striped(np.random.permutation(T)[:J]),
        "offs2": striped(np.random.permutation(T)[:J]),
    }


def reference(tab_words, tab_scales, tab2_words, tab2_scales, wa, wb_words, wb_scales, en, offs, offs2):
    idx = unstriped(offs)
    idx2 = unstriped(offs2)
    tab_ = unpack_weight(tab_words, tab_scales, "e4m3")[:, idx]
    tab2_ = unpack_weight(tab2_words, tab2_scales, "e4m3")[:, idx2]
    wa_ = mxq(f64(wa), 0, "e4m3")
    wb_ = unpack_weight(wb_words, wb_scales, "e2m1")
    ha = wa_.T @ tab_
    hb = wb_.T @ tab2_
    h = np.abs(ha - hb)
    h_ = mxq(h, 0, "e4m3")
    en_ = mxq(f64(en), 0, "e4m3")
    y = en_.T @ h_
    return y

@@ -1,0 +1,208 @@
+from contextlib import ExitStack
+
+import concourse.mybir as mybir
+
+K, L, R, N, T, J = 512, 512, 512, 512, 1024, 512
+FLOPS = 2 * (K * R * J + L * R * J + R * N * J)
+
+F32 = mybir.dt.float32
+BF16 = mybir.dt.bfloat16
+I32 = mybir.dt.int32
+U32 = mybir.dt.uint32
+U16 = mybir.dt.uint16
+U8 = mybir.dt.uint8
+FP8X4 = mybir.dt.float8_e4m3fn_x4
+FP4X4 = mybir.dt.float4_e2m1fn_x4
+ACT = mybir.ActivationFunctionType
+
+P = 128
+PACK = 4
+JC = 128
+CHUNKS = J // JC
+HALF = 256
+J_PIECES = ((0, 256), (256, 128), (384, 128))
+
+
+def tile_list_kg_absd_none_kernel(tc, tab_words, tab_scales, tab2_words, tab2_scales, wa, wb_words, wb_scales, en, offs, offs2, out):
+    nc = tc.nc
+    with ExitStack() as ctx:
+        keep = ctx.enter_context(tc.tile_pool(name="keep", bufs=1))
+        rounded = ctx.enter_context(tc.tile_pool(name="rounded", bufs=1))
+        psum = ctx.enter_context(tc.psum_pool(name="psum", bufs=8))
+
+        def load_scale_rows(engine, tile, scales):
+            rows = scales[0].bitcast(I32)
+            for quad in range(4):
+                engine.dma_start(out=tile[32 * quad : 32 * quad + 4, :], in_=rows[4 * quad : 4 * quad + 4, :])
+
+        list_a = keep.tile([P, J // 16], U16)
+        list_b = keep.tile([P, J // 16], U16)
+        tab_a_scales = keep.tile([P, T // 4], I32, align_bytes=64)
+        tab_b_scales = keep.tile([P, T // 4], I32, align_bytes=64)
+        wb_scales_raw = keep.tile([P, R // 4], I32, align_bytes=64)
+        tab_a_words = keep.tile([P, T], I32, align_bytes=64)
+        tab_b_words = keep.tile([P, T], I32, align_bytes=64)
+        wb_words_raw = keep.tile([P, R // 2], I32, align_bytes=64)
+        warm_in = keep.tile([P, 8], F32)
+        warm_out = keep.tile([P, 8], F32)
+
+        nc.vector.memset(tab_a_scales[:], 0)
+        nc.vector.memset(tab_b_scales[:], 0)
+        nc.vector.memset(wb_scales_raw[:], 0)
+        nc.vector.memset(warm_in[:], 0.0)
+        nc.scalar.activation(out=warm_out[:], in_=warm_in[:], func=ACT.Abs)
+
+        wa_rows = wa.rearrange("(p i) r -> p i r", i=PACK)
+        wa_raw = [keep.tile([P, PACK, HALF], F32, name="wa_raw_%d" % half) for half in range(2)]
+        nc.sync.dma_start(list_a[:], offs)
+        nc.sync.dma_start(list_b[:], offs2)
+        load_scale_rows(nc.sync, tab_a_scales, tab_scales)
+        nc.sync.dma_start(out=tab_a_words[:], in_=tab_words[0].rearrange("p t i -> p (t i)").bitcast(I32))
+        nc.sync.dma_start(out=wa_raw[0][:], in_=wa_rows[:, :, 0:HALF])
+        load_scale_rows(nc.sync, tab_b_scales, tab2_scales)
+        nc.sync.dma_start(out=wa_raw[1][:], in_=wa_rows[:, :, HALF : 2 * HALF])
+        load_scale_rows(nc.sync, wb_scales_raw, wb_scales)
+        nc.sync.dma_start(out=wb_words_raw[:], in_=wb_words[0].bitcast(I32))
+        nc.sync.dma_start(out=tab_b_words[:], in_=tab2_words[0].rearrange("p t i -> p (t i)").bitcast(I32))
+
+        wa_bf = rounded.tile([P, PACK, 32, 4, PACK], BF16, name="weight_bf", align_bytes=64)
+        for half in range(2):
+            src = wa_raw[half][:].rearrange("p i (g t b) -> p t g i b", t=PACK, b=4)
+            for t in range(PACK):
+                nc.scalar.activation(
+                    out=wa_bf[:, t, 16 * half : 16 * half + 16, :, :].rearrange("p g b i -> p g i b"),
+                    in_=src[:, t],
+                    func=ACT.Copy,
+                    scale=-1.0,
+                )
+
+        a_scales = keep.tile([P, J], U8, align_bytes=64)
+        a_words = keep.tile([P, J], U32, align_bytes=64)
+        b_scales = keep.tile([P, J], U8, align_bytes=64)
+        b_words = keep.tile([P, J], U32, align_bytes=64)
+        nc.vector.tensor_copy(a_scales[:], tab_a_scales[:].bitcast(U8).indirect(list_a[:]))
+        nc.vector.tensor_copy(a_words[:], tab_a_words[:].bitcast(U32).indirect(list_a[:]))
+        nc.vector.tensor_copy(b_scales[:], tab_b_scales[:].bitcast(U8).indirect(list_b[:]))
+
+        wa_codes = keep.tile([P, R], U32, align_bytes=64)
+        wa_scales = keep.tile([P, R], U8, align_bytes=64)
+        for pair in range(2):
+            cols = slice(HALF * pair, HALF * (pair + 1))
+            nc.vector.quantize_mx(
+                out=wa_codes[:, cols].bitcast(FP8X4),
+                scales=wa_scales[:, cols],
+                in_=wa_bf[:, 2 * pair : 2 * pair + 2].rearrange("p t g b i -> p (t g b i)"),
+            )
+
+        wb_codes = keep.tile([P, 2 * R], U8, align_bytes=64)
+        wb_plane = keep.tile([P, R], U8, align_bytes=64)
+        nc.vector.tensor_copy(
+            out=wb_codes[:].bitcast(I32).rearrange("p (t g w) -> p t g w", t=PACK, w=2),
+            in_=wb_words_raw[:].rearrange("p (g t w) -> p t g w", t=PACK, w=2),
+        )
+        nc.vector.tensor_copy(
+            out=wb_plane[:].bitcast(I32).rearrange("p (t g) -> p t g", t=PACK),
+            in_=wb_scales_raw[:].rearrange("p (g t) -> p t g", t=PACK),
+        )
+
+        h_bf = keep.tile([P, J, PACK], BF16, align_bytes=64)
+        h_codes = keep.tile([P, J], U32, align_bytes=64)
+        h_scales = keep.tile([P, J], U8, align_bytes=64)
+        for c in range(CHUNKS):
+            js = slice(JC * c, JC * (c + 1))
+            nc.vector.tensor_copy(
+                b_words[:, js], tab_b_words[:].bitcast(U32).indirect(list_b[:, JC // 16 * c : JC // 16 * (c + 1)])
+            )
+
+        def project(c):
+            js = slice(JC * c, JC * (c + 1))
+            diff = psum.tile([P, PACK, JC], F32, name="bank")
+            for t in range(PACK):
+                cols = slice(P * t, P * (t + 1))
+                nc.tensor.matmul_mx(
+                    out=diff[:, t, :],
+                    lhsT=wa_codes[:, cols].bitcast(FP8X4),
+                    lhsT_scale=wa_scales[:, cols],
+                    rhs=a_words[:, js].bitcast(FP8X4),
+                    rhs_scale=a_scales[:, js],
+                    start=True,
+                    stop=False,
+                )
+                nc.tensor.matmul_mx(
+                    out=diff[:, t, :],
+                    lhsT=wb_codes[:, 2 * P * t : 2 * P * (t + 1)].bitcast(FP4X4),
+                    lhsT_scale=wb_plane[:, cols],
+                    rhs=b_words[:, js].bitcast(FP8X4),
+                    rhs_scale=b_scales[:, js],
+                    start=False,
+                    stop=True,
+                )
+            nc.scalar.activation(out=h_bf[:, js, :], in_=diff[:].rearrange("p t j -> p j t"), func=ACT.Abs)
+            nc.vector.quantize_mx(
+                out=h_codes[:, js].bitcast(FP8X4),
+                scales=h_scales[:, js],
+                in_=h_bf[:, js, :].rearrange("p j t -> p (j t)"),
+            )
+
+        en_rows = en.rearrange("(g t b) n -> t g b n", t=PACK, b=4)
+        en_bf = rounded.tile([P, N, PACK], BF16, name="weight_bf", align_bytes=64)
+        en_codes = keep.tile([P, N], U32, align_bytes=64)
+        en_scales = keep.tile([P, N], U8, align_bytes=64)
+
+        def quantize_en(half):
+            ns = slice(HALF * half, HALF * (half + 1))
+            en_raw = keep.tile([P, PACK, HALF], F32, name="en_raw_%d" % half)
+            for t in range(PACK):
+                nc.sync.dma_start(out=en_raw[:, t, :], in_=en_rows[t][:, :, ns])
+            if half == 0:
+                for m in range(2):
+                    nc.scalar.copy(
+                        out=en_bf[:, P * m : P * (m + 1), :].rearrange("p (c u) t -> p c t u", u=4),
+                        in_=en_raw[:, :, P * m : P * (m + 1)].rearrange("p t (c u) -> p c t u", u=4),
+                    )
+            else:
+                nc.vector.tensor_copy(
+                    out=en_bf[:, ns, :].rearrange("p (c u) t -> p c t u", u=4),
+                    in_=en_raw[:].rearrange("p t (c u) -> p c t u", u=4),
+                )
+            nc.vector.quantize_mx(
+                out=en_codes[:, ns].bitcast(FP8X4),
+                scales=en_scales[:, ns],
+                in_=en_bf[:, ns, :].rearrange("p n t -> p (n t)"),
+            )
+
+        out_rows = out.rearrange("(m p) j -> p m j", p=P)
+
+        def score(piece, half):
+            j0, width = J_PIECES[piece]
+            js = slice(j0, j0 + width)
+            y = psum.tile([P, 2, width], F32, name="bank")
+            for m in range(2):
+                cols = slice(HALF * half + P * m, HALF * half + P * (m + 1))
+                nc.tensor.matmul_mx(
+                    out=y[:, m, :],
+                    lhsT=en_codes[:, cols].bitcast(FP8X4),
+                    lhsT_scale=en_scales[:, cols],
+                    rhs=h_codes[:, js].bitcast(FP8X4),
+                    rhs_scale=h_scales[:, js],
+                    start=True,
+                    stop=True,
+                )
+            staged = keep.tile([P, 2, width], F32, name="staged_%d_%d" % (piece, half))
+            if half == 1:
+                nc.scalar.copy(out=staged[:], in_=y[:])
+            else:
+                nc.vector.tensor_copy(out=staged[:], in_=y[:])
+            nc.sync.dma_start(out=out_rows[:, 2 * half : 2 * half + 2, js], in_=staged[:])
+
+        project(0)
+        quantize_en(0)
+        project(1)
+        quantize_en(1)
+        project(2)
+        score(0, 0)
+        project(3)
+        score(0, 1)
+        for piece in (1, 2):
+            for half in range(2):
+                score(piece, half)

@@ -28,6 +28,7 @@ def tile_list_kg_absd_none_kernel(tc, tab_words, tab_scales, tab2_words, tab2_sc
     with ExitStack() as ctx:
         keep = ctx.enter_context(tc.tile_pool(name="keep", bufs=1))
         rounded = ctx.enter_context(tc.tile_pool(name="rounded", bufs=1))
+        stage = ctx.enter_context(tc.tile_pool(name="stage", bufs=2))
         psum = ctx.enter_context(tc.psum_pool(name="psum", bufs=8))
 
         def load_scale_rows(engine, tile, scales):
@@ -60,21 +61,19 @@ def tile_list_kg_absd_none_kernel(tc, tab_words, tab_scales, tab2_words, tab2_sc
         nc.sync.dma_start(out=tab_a_words[:], in_=tab_words[0].rearrange("p t i -> p (t i)").bitcast(I32))
         nc.sync.dma_start(out=wa_raw[0][:], in_=wa_rows[:, :, 0:HALF])
         load_scale_rows(nc.sync, tab_b_scales, tab2_scales)
-        nc.sync.dma_start(out=wa_raw[1][:], in_=wa_rows[:, :, HALF : 2 * HALF])
-        load_scale_rows(nc.sync, wb_scales_raw, wb_scales)
         nc.sync.dma_start(out=wb_words_raw[:], in_=wb_words[0].bitcast(I32))
+        nc.sync.dma_start(out=wa_raw[1][:], in_=wa_rows[:, :, HALF : 2 * HALF])
         nc.sync.dma_start(out=tab_b_words[:], in_=tab2_words[0].rearrange("p t i -> p (t i)").bitcast(I32))
+        load_scale_rows(nc.sync, wb_scales_raw, wb_scales)
 
-        wa_bf = rounded.tile([P, PACK, 32, 4, PACK], BF16, name="weight_bf", align_bytes=64)
+        wa_bf = rounded.tile([P, PACK, P, PACK], BF16, name="weight_bf", align_bytes=64)
         for half in range(2):
-            src = wa_raw[half][:].rearrange("p i (g t b) -> p t g i b", t=PACK, b=4)
-            for t in range(PACK):
-                nc.scalar.activation(
-                    out=wa_bf[:, t, 16 * half : 16 * half + 16, :, :].rearrange("p g b i -> p g i b"),
-                    in_=src[:, t],
-                    func=ACT.Copy,
-                    scale=-1.0,
-                )
+            nc.scalar.activation(
+                out=wa_bf[:, :, 64 * half : 64 * half + 64, :].rearrange("p t m i -> p m i t"),
+                in_=wa_raw[half][:].rearrange("p i (m t) -> p m i t", t=PACK),
+                func=ACT.Copy,
+                scale=-1.0,
+            )
 
         a_scales = keep.tile([P, J], U8, align_bytes=64)
         a_words = keep.tile([P, J], U32, align_bytes=64)
@@ -86,35 +85,27 @@ def tile_list_kg_absd_none_kernel(tc, tab_words, tab_scales, tab2_words, tab2_sc
 
         wa_codes = keep.tile([P, R], U32, align_bytes=64)
         wa_scales = keep.tile([P, R], U8, align_bytes=64)
-        for pair in range(2):
-            cols = slice(HALF * pair, HALF * (pair + 1))
-            nc.vector.quantize_mx(
-                out=wa_codes[:, cols].bitcast(FP8X4),
-                scales=wa_scales[:, cols],
-                in_=wa_bf[:, 2 * pair : 2 * pair + 2].rearrange("p t g b i -> p (t g b i)"),
-            )
+        nc.vector.quantize_mx(
+            out=wa_codes[:].bitcast(FP8X4), scales=wa_scales[:], in_=wa_bf[:].rearrange("p t m i -> p (t m i)")
+        )
 
         wb_codes = keep.tile([P, 2 * R], U8, align_bytes=64)
         wb_plane = keep.tile([P, R], U8, align_bytes=64)
         nc.vector.tensor_copy(
-            out=wb_codes[:].bitcast(I32).rearrange("p (t g w) -> p t g w", t=PACK, w=2),
-            in_=wb_words_raw[:].rearrange("p (g t w) -> p t g w", t=PACK, w=2),
+            out=wb_codes[:].bitcast(U16).rearrange("p (t m) -> p t m", t=PACK),
+            in_=wb_words_raw[:].bitcast(U16).rearrange("p (m t) -> p t m", t=PACK),
         )
         nc.vector.tensor_copy(
-            out=wb_plane[:].bitcast(I32).rearrange("p (t g) -> p t g", t=PACK),
-            in_=wb_scales_raw[:].rearrange("p (g t) -> p t g", t=PACK),
+            out=wb_plane[:].rearrange("p (t m) -> p m t", t=PACK),
+            in_=wb_scales_raw[:].bitcast(U8).rearrange("p (m t) -> p m t", t=PACK),
         )
 
-        h_bf = keep.tile([P, J, PACK], BF16, align_bytes=64)
         h_codes = keep.tile([P, J], U32, align_bytes=64)
         h_scales = keep.tile([P, J], U8, align_bytes=64)
-        for c in range(CHUNKS):
-            js = slice(JC * c, JC * (c + 1))
-            nc.vector.tensor_copy(
-                b_words[:, js], tab_b_words[:].bitcast(U32).indirect(list_b[:, JC // 16 * c : JC // 16 * (c + 1)])
-            )
+        for j0, j1 in ((0, 128), (128, 256), (256, 512)):
+            nc.vector.tensor_copy(b_words[:, j0:j1], tab_b_words[:].bitcast(U32).indirect(list_b[:, j0 // 16 : j1 // 16]))
 
-        def project(c):
+        def project(c, h_bf):
             js = slice(JC * c, JC * (c + 1))
             diff = psum.tile([P, PACK, JC], F32, name="bank")
             for t in range(PACK):
@@ -137,34 +128,32 @@ def tile_list_kg_absd_none_kernel(tc, tab_words, tab_scales, tab2_words, tab2_sc
                     start=False,
                     stop=True,
                 )
-            nc.scalar.activation(out=h_bf[:, js, :], in_=diff[:].rearrange("p t j -> p j t"), func=ACT.Abs)
+            nc.scalar.activation(out=h_bf, in_=diff[:].rearrange("p t j -> p j t"), func=ACT.Abs)
             nc.vector.quantize_mx(
                 out=h_codes[:, js].bitcast(FP8X4),
                 scales=h_scales[:, js],
-                in_=h_bf[:, js, :].rearrange("p j t -> p (j t)"),
+                in_=h_bf.rearrange("p j t -> p (j t)"),
             )
 
-        en_rows = en.rearrange("(g t b) n -> t g b n", t=PACK, b=4)
+        en_rows = en.rearrange("(p t) n -> p t n", t=PACK)
         en_bf = rounded.tile([P, N, PACK], BF16, name="weight_bf", align_bytes=64)
         en_codes = keep.tile([P, N], U32, align_bytes=64)
         en_scales = keep.tile([P, N], U8, align_bytes=64)
 
         def quantize_en(half):
             ns = slice(HALF * half, HALF * (half + 1))
-            en_raw = keep.tile([P, PACK, HALF], F32, name="en_raw_%d" % half)
-            for t in range(PACK):
-                nc.sync.dma_start(out=en_raw[:, t, :], in_=en_rows[t][:, :, ns])
-            if half == 0:
-                for m in range(2):
-                    nc.scalar.copy(
-                        out=en_bf[:, P * m : P * (m + 1), :].rearrange("p (c u) t -> p c t u", u=4),
-                        in_=en_raw[:, :, P * m : P * (m + 1)].rearrange("p t (c u) -> p c t u", u=4),
-                    )
-            else:
-                nc.vector.tensor_copy(
-                    out=en_bf[:, ns, :].rearrange("p (c u) t -> p c t u", u=4),
-                    in_=en_raw[:].rearrange("p t (c u) -> p c t u", u=4),
+            en_raw = stage.tile([P, PACK, HALF], F32, name="stage", align_bytes=64)
+            nc.sync.dma_start(out=en_raw[:], in_=en_rows[:, :, ns])
+            on_scalar = P if half == 0 else 0
+            if on_scalar:
+                nc.scalar.copy(
+                    out=en_bf[:, 0:on_scalar, :].rearrange("p (c u) t -> p c t u", u=4),
+                    in_=en_raw[:, :, 0:on_scalar].rearrange("p t (c u) -> p c t u", u=4),
                 )
+            nc.vector.tensor_copy(
+                out=en_bf[:, HALF * half + on_scalar : HALF * (half + 1), :].rearrange("p (c u) t -> p c t u", u=4),
+                in_=en_raw[:, :, on_scalar:HALF].rearrange("p t (c u) -> p c t u", u=4),
+            )
             nc.vector.quantize_mx(
                 out=en_codes[:, ns].bitcast(FP8X4),
                 scales=en_scales[:, ns],
@@ -195,14 +184,12 @@ def tile_list_kg_absd_none_kernel(tc, tab_words, tab_scales, tab2_words, tab2_sc
                 nc.vector.tensor_copy(out=staged[:], in_=y[:])
             nc.sync.dma_start(out=out_rows[:, 2 * half : 2 * half + 2, js], in_=staged[:])
 
-        project(0)
         quantize_en(0)
-        project(1)
         quantize_en(1)
-        project(2)
-        score(0, 0)
-        project(3)
-        score(0, 1)
-        for piece in (1, 2):
+        for pair in range(2):
+            h_pair = stage.tile([P, 2 * JC, PACK], BF16, name="stage", align_bytes=64)
+            for c in range(2):
+                project(2 * pair + c, h_pair[:, JC * c : JC * (c + 1), :])
+        for piece in range(len(J_PIECES)):
             for half in range(2):
                 score(piece, half)

@@ -20,7 +20,7 @@ PACK = 4
 JC = 128
 CHUNKS = J // JC
 HALF = 256
-J_PIECES = ((0, 256), (256, 128), (384, 128))
+J_PIECES = ((0, 256), (256, 256))
 
 
 def tile_list_kg_absd_none_kernel(tc, tab_words, tab_scales, tab2_words, tab2_scales, wa, wb_words, wb_scales, en, offs, offs2, out):
@@ -29,6 +29,7 @@ def tile_list_kg_absd_none_kernel(tc, tab_words, tab_scales, tab2_words, tab2_sc
         keep = ctx.enter_context(tc.tile_pool(name="keep", bufs=1))
         rounded = ctx.enter_context(tc.tile_pool(name="rounded", bufs=1))
         stage = ctx.enter_context(tc.tile_pool(name="stage", bufs=2))
+        small = ctx.enter_context(tc.tile_pool(name="small", bufs=1))
         psum = ctx.enter_context(tc.psum_pool(name="psum", bufs=8))
 
         def load_scale_rows(engine, tile, scales):
@@ -40,7 +41,7 @@ def tile_list_kg_absd_none_kernel(tc, tab_words, tab_scales, tab2_words, tab2_sc
         list_b = keep.tile([P, J // 16], U16)
         tab_a_scales = keep.tile([P, T // 4], I32, align_bytes=64)
         tab_b_scales = keep.tile([P, T // 4], I32, align_bytes=64)
-        wb_scales_raw = keep.tile([P, R // 4], I32, align_bytes=64)
+        wb_scales_raw = small.tile([P, R // 4], I32, name="small", align_bytes=64)
         tab_a_words = keep.tile([P, T], I32, align_bytes=64)
         tab_b_words = keep.tile([P, T], I32, align_bytes=64)
         wb_words_raw = keep.tile([P, R // 2], I32, align_bytes=64)
@@ -55,34 +56,44 @@ def tile_list_kg_absd_none_kernel(tc, tab_words, tab_scales, tab2_words, tab2_sc
 
         wa_rows = wa.rearrange("(p i) r -> p i r", i=PACK)
         wa_raw = [keep.tile([P, PACK, HALF], F32, name="wa_raw_%d" % half) for half in range(2)]
+        nc.sync.dma_start(out=wb_words_raw[:], in_=wb_words[0].bitcast(I32))
         nc.sync.dma_start(list_a[:], offs)
-        nc.sync.dma_start(list_b[:], offs2)
         load_scale_rows(nc.sync, tab_a_scales, tab_scales)
         nc.sync.dma_start(out=tab_a_words[:], in_=tab_words[0].rearrange("p t i -> p (t i)").bitcast(I32))
         nc.sync.dma_start(out=wa_raw[0][:], in_=wa_rows[:, :, 0:HALF])
+        nc.sync.dma_start(list_b[:], offs2)
         load_scale_rows(nc.sync, tab_b_scales, tab2_scales)
-        nc.sync.dma_start(out=wb_words_raw[:], in_=wb_words[0].bitcast(I32))
         nc.sync.dma_start(out=wa_raw[1][:], in_=wa_rows[:, :, HALF : 2 * HALF])
         nc.sync.dma_start(out=tab_b_words[:], in_=tab2_words[0].rearrange("p t i -> p (t i)").bitcast(I32))
         load_scale_rows(nc.sync, wb_scales_raw, wb_scales)
 
         wa_bf = rounded.tile([P, PACK, P, PACK], BF16, name="weight_bf", align_bytes=64)
-        for half in range(2):
-            nc.scalar.activation(
-                out=wa_bf[:, :, 64 * half : 64 * half + 64, :].rearrange("p t m i -> p m i t"),
-                in_=wa_raw[half][:].rearrange("p i (m t) -> p m i t", t=PACK),
-                func=ACT.Copy,
-                scale=-1.0,
-            )
+        nc.scalar.activation(
+            out=wa_bf[:, :, 0:64, :].rearrange("p t m i -> p m i t"),
+            in_=wa_raw[0][:].rearrange("p i (m t) -> p m i t", t=PACK),
+            func=ACT.Copy,
+            scale=-1.0,
+        )
+        nc.scalar.activation(
+            out=wa_bf[:, :, 64:96, :].rearrange("p t m i -> p m i t"),
+            in_=wa_raw[1][:, :, 0:P].rearrange("p i (m t) -> p m i t", t=PACK),
+            func=ACT.Copy,
+            scale=-1.0,
+        )
 
         a_scales = keep.tile([P, J], U8, align_bytes=64)
         a_words = keep.tile([P, J], U32, align_bytes=64)
         b_scales = keep.tile([P, J], U8, align_bytes=64)
-        b_words = keep.tile([P, J], U32, align_bytes=64)
+        b_first = keep.tile([P, JC], U32, align_bytes=64)
         nc.vector.tensor_copy(a_scales[:], tab_a_scales[:].bitcast(U8).indirect(list_a[:]))
         nc.vector.tensor_copy(a_words[:], tab_a_words[:].bitcast(U32).indirect(list_a[:]))
         nc.vector.tensor_copy(b_scales[:], tab_b_scales[:].bitcast(U8).indirect(list_b[:]))
 
+        nc.vector.tensor_scalar_mul(
+            wa_bf[:, :, 96:128, :].rearrange("p t m i -> p m i t"),
+            wa_raw[1][:, :, P:HALF].rearrange("p i (m t) -> p m i t", t=PACK),
+            -1.0,
+        )
         wa_codes = keep.tile([P, R], U32, align_bytes=64)
         wa_scales = keep.tile([P, R], U8, align_bytes=64)
         nc.vector.quantize_mx(
@@ -100,10 +111,14 @@ def tile_list_kg_absd_none_kernel(tc, tab_words, tab_scales, tab2_words, tab2_sc
             in_=wb_scales_raw[:].bitcast(U8).rearrange("p (m t) -> p m t", t=PACK),
         )
 
-        h_codes = keep.tile([P, J], U32, align_bytes=64)
         h_scales = keep.tile([P, J], U8, align_bytes=64)
-        for j0, j1 in ((0, 128), (128, 256), (256, 512)):
-            nc.vector.tensor_copy(b_words[:, j0:j1], tab_b_words[:].bitcast(U32).indirect(list_b[:, j0 // 16 : j1 // 16]))
+        nc.vector.tensor_copy(b_first[:], tab_b_words[:].bitcast(U32).indirect(list_b[:, 0 : JC // 16]))
+        b_rest = small.tile([P, J - JC], U32, name="small", align_bytes=64)
+        for j0, j1 in ((128, 256), (256, 512)):
+            nc.vector.tensor_copy(
+                b_rest[:, j0 - JC : j1 - JC], tab_b_words[:].bitcast(U32).indirect(list_b[:, j0 // 16 : j1 // 16])
+            )
+        b_words = [b_first[:]] + [b_rest[:, JC * c : JC * (c + 1)] for c in range(CHUNKS - 1)]
 
         def project(c, h_bf):
             js = slice(JC * c, JC * (c + 1))
@@ -123,7 +138,7 @@ def tile_list_kg_absd_none_kernel(tc, tab_words, tab_scales, tab2_words, tab2_sc
                     out=diff[:, t, :],
                     lhsT=wb_codes[:, 2 * P * t : 2 * P * (t + 1)].bitcast(FP4X4),
                     lhsT_scale=wb_plane[:, cols],
-                    rhs=b_words[:, js].bitcast(FP8X4),
+                    rhs=b_words[c].bitcast(FP8X4),
                     rhs_scale=b_scales[:, js],
                     start=False,
                     stop=True,
@@ -178,7 +193,7 @@ def tile_list_kg_absd_none_kernel(tc, tab_words, tab_scales, tab2_words, tab2_sc
                     stop=True,
                 )
             staged = keep.tile([P, 2, width], F32, name="staged_%d_%d" % (piece, half))
-            if half == 1:
+            if half == 0:
                 nc.scalar.copy(out=staged[:], in_=y[:])
             else:
                 nc.vector.tensor_copy(out=staged[:], in_=y[:])
@@ -186,10 +201,10 @@ def tile_list_kg_absd_none_kernel(tc, tab_words, tab_scales, tab2_words, tab2_sc
 
         quantize_en(0)
         quantize_en(1)
-        for pair in range(2):
-            h_pair = stage.tile([P, 2 * JC, PACK], BF16, name="stage", align_bytes=64)
-            for c in range(2):
-                project(2 * pair + c, h_pair[:, JC * c : JC * (c + 1), :])
+        h_all = stage.tile([P, J, PACK], BF16, name="stage", align_bytes=64)
+        h_codes = stage.tile([P, J], U32, name="stage", align_bytes=64)
+        for c in range(CHUNKS):
+            project(c, h_all[:, JC * c : JC * (c + 1), :])
         for piece in range(len(J_PIECES)):
             for half in range(2):
                 score(piece, half)

@@ -20,7 +20,6 @@ PACK = 4
 JC = 128
 CHUNKS = J // JC
 HALF = 256
-J_PIECES = ((0, 256), (256, 256))
 
 
 def tile_list_kg_absd_none_kernel(tc, tab_words, tab_scales, tab2_words, tab2_scales, wa, wb_words, wb_scales, en, offs, offs2, out):
@@ -144,6 +143,9 @@ def tile_list_kg_absd_none_kernel(tc, tab_words, tab_scales, tab2_words, tab2_sc
                     stop=True,
                 )
             nc.scalar.activation(out=h_bf, in_=diff[:].rearrange("p t j -> p j t"), func=ACT.Abs)
+
+        def quantize_h(c, h_bf):
+            js = slice(JC * c, JC * (c + 1))
             nc.vector.quantize_mx(
                 out=h_codes[:, js].bitcast(FP8X4),
                 scales=h_scales[:, js],
@@ -155,10 +157,9 @@ def tile_list_kg_absd_none_kernel(tc, tab_words, tab_scales, tab2_words, tab2_sc
         en_codes = keep.tile([P, N], U32, align_bytes=64)
         en_scales = keep.tile([P, N], U8, align_bytes=64)
 
-        def quantize_en(half):
-            ns = slice(HALF * half, HALF * (half + 1))
+        def round_en(half):
             en_raw = stage.tile([P, PACK, HALF], F32, name="stage", align_bytes=64)
-            nc.sync.dma_start(out=en_raw[:], in_=en_rows[:, :, ns])
+            nc.sync.dma_start(out=en_raw[:], in_=en_rows[:, :, HALF * half : HALF * (half + 1)])
             on_scalar = P if half == 0 else 0
             if on_scalar:
                 nc.scalar.copy(
@@ -169,42 +170,50 @@ def tile_list_kg_absd_none_kernel(tc, tab_words, tab_scales, tab2_words, tab2_sc
                 out=en_bf[:, HALF * half + on_scalar : HALF * (half + 1), :].rearrange("p (c u) t -> p c t u", u=4),
                 in_=en_raw[:, :, on_scalar:HALF].rearrange("p t (c u) -> p c t u", u=4),
             )
+
+        def quantize_en(half):
+            ns = slice(HALF * half, HALF * (half + 1))
             nc.vector.quantize_mx(
                 out=en_codes[:, ns].bitcast(FP8X4),
                 scales=en_scales[:, ns],
                 in_=en_bf[:, ns, :].rearrange("p n t -> p (n t)"),
             )
 
-        out_rows = out.rearrange("(m p) j -> p m j", p=P)
-
-        def score(piece, half):
-            j0, width = J_PIECES[piece]
-            js = slice(j0, j0 + width)
-            y = psum.tile([P, 2, width], F32, name="bank")
-            for m in range(2):
-                cols = slice(HALF * half + P * m, HALF * half + P * (m + 1))
-                nc.tensor.matmul_mx(
-                    out=y[:, m, :],
-                    lhsT=en_codes[:, cols].bitcast(FP8X4),
-                    lhsT_scale=en_scales[:, cols],
-                    rhs=h_codes[:, js].bitcast(FP8X4),
-                    rhs_scale=h_scales[:, js],
-                    start=True,
-                    stop=True,
-                )
-            staged = keep.tile([P, 2, width], F32, name="staged_%d_%d" % (piece, half))
-            if half == 0:
-                nc.scalar.copy(out=staged[:], in_=y[:])
-            else:
+        def score(j_half, m, on_vector):
+            js = slice(HALF * j_half, HALF * (j_half + 1))
+            ns = slice(P * m, P * (m + 1))
+            y = psum.tile([P, HALF], F32, name="bank")
+            nc.tensor.matmul_mx(
+                out=y[:],
+                lhsT=en_codes[:, ns].bitcast(FP8X4),
+                lhsT_scale=en_scales[:, ns],
+                rhs=h_codes[:, js].bitcast(FP8X4),
+                rhs_scale=h_scales[:, js],
+                start=True,
+                stop=True,
+            )
+            staged = keep.tile([P, HALF], F32, name="staged_%d_%d" % (j_half, m))
+            if on_vector:
                 nc.vector.tensor_copy(out=staged[:], in_=y[:])
-            nc.sync.dma_start(out=out_rows[:, 2 * half : 2 * half + 2, js], in_=staged[:])
+            else:
+                nc.scalar.copy(out=staged[:], in_=y[:])
+            nc.sync.dma_start(out=out[ns, js], in_=staged[:])
 
+        round_en(0)
         quantize_en(0)
-        quantize_en(1)
+        round_en(1)
         h_all = stage.tile([P, J, PACK], BF16, name="stage", align_bytes=64)
         h_codes = stage.tile([P, J], U32, name="stage", align_bytes=64)
+        h_chunks = [h_all[:, JC * c : JC * (c + 1), :] for c in range(CHUNKS)]
         for c in range(CHUNKS):
-            project(c, h_all[:, JC * c : JC * (c + 1), :])
-        for piece in range(len(J_PIECES)):
-            for half in range(2):
-                score(piece, half)
+            project(c, h_chunks[c])
+        quantize_h(0, h_chunks[0])
+        quantize_h(1, h_chunks[1])
+        quantize_en(1)
+        quantize_h(2, h_chunks[2])
+        score(0, 0, True)
+        quantize_h(3, h_chunks[3])
+        for m in range(1, 4):
+            score(0, m, m % 2 == 0)
+        for m in range(4):
+            score(1, m, m % 2 == 1)

@@ -20,200 +20,182 @@ PACK = 4
 JC = 128
 CHUNKS = J // JC
 HALF = 256
+MH = HALF // PACK
 
 
 def tile_list_kg_absd_none_kernel(tc, tab_words, tab_scales, tab2_words, tab2_scales, wa, wb_words, wb_scales, en, offs, offs2, out):
     nc = tc.nc
     with ExitStack() as ctx:
         keep = ctx.enter_context(tc.tile_pool(name="keep", bufs=1))
-        rounded = ctx.enter_context(tc.tile_pool(name="rounded", bufs=1))
-        stage = ctx.enter_context(tc.tile_pool(name="stage", bufs=2))
-        small = ctx.enter_context(tc.tile_pool(name="small", bufs=1))
+        reuse = ctx.enter_context(tc.tile_pool(name="reuse", bufs=1))
         psum = ctx.enter_context(tc.psum_pool(name="psum", bufs=8))
 
-        def load_scale_rows(engine, tile, scales):
+        def load_scale_rows(engines, tile, scales):
             rows = scales[0].bitcast(I32)
             for quad in range(4):
-                engine.dma_start(out=tile[32 * quad : 32 * quad + 4, :], in_=rows[4 * quad : 4 * quad + 4, :])
+                engines[quad].dma_start(out=tile[32 * quad : 32 * quad + 4, :], in_=rows[4 * quad : 4 * quad + 4, :])
 
         list_a = keep.tile([P, J // 16], U16)
         list_b = keep.tile([P, J // 16], U16)
         tab_a_scales = keep.tile([P, T // 4], I32, align_bytes=64)
         tab_b_scales = keep.tile([P, T // 4], I32, align_bytes=64)
-        wb_scales_raw = small.tile([P, R // 4], I32, name="small", align_bytes=64)
+        wb_scales_raw = keep.tile([P, R // 4], I32, align_bytes=64)
         tab_a_words = keep.tile([P, T], I32, align_bytes=64)
         tab_b_words = keep.tile([P, T], I32, align_bytes=64)
         wb_words_raw = keep.tile([P, R // 2], I32, align_bytes=64)
-        warm_in = keep.tile([P, 8], F32)
-        warm_out = keep.tile([P, 8], F32)
 
-        nc.vector.memset(tab_a_scales[:], 0)
         nc.vector.memset(tab_b_scales[:], 0)
         nc.vector.memset(wb_scales_raw[:], 0)
-        nc.vector.memset(warm_in[:], 0.0)
-        nc.scalar.activation(out=warm_out[:], in_=warm_in[:], func=ACT.Abs)
+        nc.vector.memset(tab_a_scales[:], 0)
 
         wa_rows = wa.rearrange("(p i) r -> p i r", i=PACK)
-        wa_raw = [keep.tile([P, PACK, HALF], F32, name="wa_raw_%d" % half) for half in range(2)]
-        nc.sync.dma_start(out=wb_words_raw[:], in_=wb_words[0].bitcast(I32))
-        nc.sync.dma_start(list_a[:], offs)
-        load_scale_rows(nc.sync, tab_a_scales, tab_scales)
-        nc.sync.dma_start(out=tab_a_words[:], in_=tab_words[0].rearrange("p t i -> p (t i)").bitcast(I32))
-        nc.sync.dma_start(out=wa_raw[0][:], in_=wa_rows[:, :, 0:HALF])
+        en_rows = en.rearrange("(p t) n -> p t n", t=PACK)
+        wa_raw = [keep.tile([P, PACK, 512], F32, name="wa_raw_0")]
+        en_raw = [keep.tile([P, PACK, 256], F32, name="en_raw_0"), keep.tile([P, PACK, 256], F32, name="en_raw_1")]
         nc.sync.dma_start(list_b[:], offs2)
-        load_scale_rows(nc.sync, tab_b_scales, tab2_scales)
-        nc.sync.dma_start(out=wa_raw[1][:], in_=wa_rows[:, :, HALF : 2 * HALF])
+        nc.sync.dma_start(out=wb_words_raw[:], in_=wb_words[0].bitcast(I32))
+        load_scale_rows((nc.sync, nc.sync, nc.scalar, nc.scalar), tab_b_scales, tab2_scales)
         nc.sync.dma_start(out=tab_b_words[:], in_=tab2_words[0].rearrange("p t i -> p (t i)").bitcast(I32))
-        load_scale_rows(nc.sync, wb_scales_raw, wb_scales)
+        nc.sync.dma_start(out=tab_a_words[:], in_=tab_words[0].rearrange("p t i -> p (t i)").bitcast(I32))
+        load_scale_rows((nc.sync, nc.sync, nc.sync, nc.sync), wb_scales_raw, wb_scales)
+        nc.sync.dma_start(list_a[:], offs)
+        nc.sync.dma_start(out=wa_raw[0][:], in_=wa_rows[:, :, 0 : 512])
+        load_scale_rows((nc.sync, nc.sync, nc.sync, nc.sync), tab_a_scales, tab_scales)
+        nc.sync.dma_start(out=en_raw[0][:], in_=en_rows[:, :, 0 : 256])
+        nc.sync.dma_start(out=en_raw[1][:], in_=en_rows[:, :, 256 : 512])
 
-        wa_bf = rounded.tile([P, PACK, P, PACK], BF16, name="weight_bf", align_bytes=64)
-        nc.scalar.activation(
-            out=wa_bf[:, :, 0:64, :].rearrange("p t m i -> p m i t"),
-            in_=wa_raw[0][:].rearrange("p i (m t) -> p m i t", t=PACK),
-            func=ACT.Copy,
-            scale=-1.0,
-        )
-        nc.scalar.activation(
-            out=wa_bf[:, :, 64:96, :].rearrange("p t m i -> p m i t"),
-            in_=wa_raw[1][:, :, 0:P].rearrange("p i (m t) -> p m i t", t=PACK),
-            func=ACT.Copy,
-            scale=-1.0,
-        )
+        wa_bf = keep.tile([P, PACK, P, PACK], BF16, align_bytes=64)
+        nc.scalar.activation(out=wa_bf[:, :, 0 : 44, :].rearrange("p t m i -> p m i t"), in_=wa_raw[0][:, :, 0 : 176].rearrange("p i (m t) -> p m i t", t=PACK), func=ACT.Copy, scale=-1.0)
 
-        a_scales = keep.tile([P, J], U8, align_bytes=64)
-        a_words = keep.tile([P, J], U32, align_bytes=64)
         b_scales = keep.tile([P, J], U8, align_bytes=64)
-        b_first = keep.tile([P, JC], U32, align_bytes=64)
-        nc.vector.tensor_copy(a_scales[:], tab_a_scales[:].bitcast(U8).indirect(list_a[:]))
-        nc.vector.tensor_copy(a_words[:], tab_a_words[:].bitcast(U32).indirect(list_a[:]))
-        nc.vector.tensor_copy(b_scales[:], tab_b_scales[:].bitcast(U8).indirect(list_b[:]))
-
-        nc.vector.tensor_scalar_mul(
-            wa_bf[:, :, 96:128, :].rearrange("p t m i -> p m i t"),
-            wa_raw[1][:, :, P:HALF].rearrange("p i (m t) -> p m i t", t=PACK),
-            -1.0,
-        )
-        wa_codes = keep.tile([P, R], U32, align_bytes=64)
-        wa_scales = keep.tile([P, R], U8, align_bytes=64)
-        nc.vector.quantize_mx(
-            out=wa_codes[:].bitcast(FP8X4), scales=wa_scales[:], in_=wa_bf[:].rearrange("p t m i -> p (t m i)")
-        )
-
+        b_words = keep.tile([P, J], U32, align_bytes=64)
         wb_codes = keep.tile([P, 2 * R], U8, align_bytes=64)
         wb_plane = keep.tile([P, R], U8, align_bytes=64)
         nc.vector.tensor_copy(
             out=wb_codes[:].bitcast(U16).rearrange("p (t m) -> p t m", t=PACK),
             in_=wb_words_raw[:].bitcast(U16).rearrange("p (m t) -> p t m", t=PACK),
         )
+        nc.vector.tensor_copy(b_scales[:], tab_b_scales[:].bitcast(U8).indirect(list_b[:]))
+        nc.vector.tensor_copy(b_words[:], tab_b_words[:].bitcast(U32).indirect(list_b[:]))
         nc.vector.tensor_copy(
             out=wb_plane[:].rearrange("p (t m) -> p m t", t=PACK),
             in_=wb_scales_raw[:].bitcast(U8).rearrange("p (m t) -> p m t", t=PACK),
         )
 
-        h_scales = keep.tile([P, J], U8, align_bytes=64)
-        nc.vector.tensor_copy(b_first[:], tab_b_words[:].bitcast(U32).indirect(list_b[:, 0 : JC // 16]))
-        b_rest = small.tile([P, J - JC], U32, name="small", align_bytes=64)
-        for j0, j1 in ((128, 256), (256, 512)):
-            nc.vector.tensor_copy(
-                b_rest[:, j0 - JC : j1 - JC], tab_b_words[:].bitcast(U32).indirect(list_b[:, j0 // 16 : j1 // 16])
-            )
-        b_words = [b_first[:]] + [b_rest[:, JC * c : JC * (c + 1)] for c in range(CHUNKS - 1)]
+        diff = [psum.tile([P, PACK, JC], F32, name="bank") for c in range(CHUNKS)]
 
-        def project(c, h_bf):
+        def project_b(c):
             js = slice(JC * c, JC * (c + 1))
-            diff = psum.tile([P, PACK, JC], F32, name="bank")
+            for t in range(PACK):
+                nc.tensor.matmul_mx(
+                    out=diff[c][:, t, :],
+                    lhsT=wb_codes[:, 2 * P * t : 2 * P * (t + 1)].bitcast(FP4X4),
+                    lhsT_scale=wb_plane[:, P * t : P * (t + 1)],
+                    rhs=b_words[:, js].bitcast(FP8X4),
+                    rhs_scale=b_scales[:, js],
+                    start=(t == 0),
+                    stop=False,
+                )
+
+        for c in range(CHUNKS):
+            project_b(c)
+
+        a_scales = keep.tile([P, J], U8, align_bytes=64)
+        wa_scales = keep.tile([P, R], U8, align_bytes=64)
+        wa_codes = keep.tile([P, R], U32, align_bytes=64)
+        a_words = keep.tile([P, J], U32, align_bytes=64)
+        nc.vector.tensor_copy(a_words[:], tab_a_words[:].bitcast(U32).indirect(list_a[:, 0 : 32]))
+        nc.vector.tensor_scalar_mul(wa_bf[:, :, 44 : 128, :].rearrange("p t m i -> p m i t"), wa_raw[0][:, :, 176 : 512].rearrange("p i (m t) -> p m i t", t=PACK), -1.0)
+        nc.vector.quantize_mx(out=wa_codes[:].bitcast(FP8X4), scales=wa_scales[:], in_=wa_bf[:].rearrange("p t m i -> p (t m i)"))
+        nc.vector.tensor_copy(a_scales[:, 0 : 128], tab_a_scales[:].bitcast(U8).indirect(list_a[:, 0 : 8]))
+        nc.vector.tensor_copy(a_scales[:, 128 : 256], tab_a_scales[:].bitcast(U8).indirect(list_a[:, 8 : 16]))
+        nc.vector.tensor_copy(a_scales[:, 256 : 384], tab_a_scales[:].bitcast(U8).indirect(list_a[:, 16 : 24]))
+        nc.vector.tensor_copy(a_scales[:, 384 : 512], tab_a_scales[:].bitcast(U8).indirect(list_a[:, 24 : 32]))
+
+        en_bf = [keep.tile([P, HALF, PACK], BF16, name="en_bf_%d" % half, align_bytes=64) for half in range(2)]
+        en_codes = keep.tile([P, N], U32, align_bytes=64)
+        en_scales = keep.tile([P, N], U8, align_bytes=64)
+        nc.scalar.copy(out=en_bf[0][:, 0 : 192, :].rearrange("p (c u) t -> p c t u", u=4), in_=en_raw[0][:, :, 0 : 192].rearrange("p t (c u) -> p c t u", u=4))
+
+        h_bf = keep.tile([P, J, PACK], BF16, align_bytes=64)
+
+        def project_a(c):
+            js = slice(JC * c, JC * (c + 1))
             for t in range(PACK):
                 cols = slice(P * t, P * (t + 1))
                 nc.tensor.matmul_mx(
-                    out=diff[:, t, :],
+                    out=diff[c][:, t, :],
                     lhsT=wa_codes[:, cols].bitcast(FP8X4),
                     lhsT_scale=wa_scales[:, cols],
                     rhs=a_words[:, js].bitcast(FP8X4),
                     rhs_scale=a_scales[:, js],
-                    start=True,
-                    stop=False,
-                )
-                nc.tensor.matmul_mx(
-                    out=diff[:, t, :],
-                    lhsT=wb_codes[:, 2 * P * t : 2 * P * (t + 1)].bitcast(FP4X4),
-                    lhsT_scale=wb_plane[:, cols],
-                    rhs=b_words[c].bitcast(FP8X4),
-                    rhs_scale=b_scales[:, js],
                     start=False,
+                    stop=(t == PACK - 1),
+                )
+
+        def rectify(c):
+            nc.scalar.activation(out=h_bf[:, JC * c : JC * (c + 1), :], in_=diff[c][:].rearrange("p t j -> p j t"), func=ACT.Abs)
+
+        for c in range(CHUNKS):
+            project_a(c)
+
+        h_codes = keep.tile([P, J], U32, align_bytes=64)
+        h_scales = keep.tile([P, J], U8, align_bytes=64)
+
+        def quantize_h(j0, j1):
+            nc.vector.quantize_mx(
+                out=h_codes[:, j0:j1].bitcast(FP8X4),
+                scales=h_scales[:, j0:j1],
+                in_=h_bf[:, j0:j1, :].rearrange("p j t -> p (j t)"),
+            )
+
+        def quantize_en(n0, n1):
+            half = n0 // HALF
+            nc.vector.quantize_mx(
+                out=en_codes[:, n0:n1].bitcast(FP8X4),
+                scales=en_scales[:, n0:n1],
+                in_=en_bf[half][:, n0 - HALF * half : n1 - HALF * half, :].rearrange("p n t -> p (n t)"),
+            )
+
+        def score(j0, width, m0, count, engine):
+            js = slice(j0, j0 + width)
+            y = psum.tile([P, count, width], F32, name="bank")
+            for m in range(count):
+                ns = slice(P * (m0 + m), P * (m0 + m + 1))
+                nc.tensor.matmul_mx(
+                    out=y[:, m, :],
+                    lhsT=en_codes[:, ns].bitcast(FP8X4),
+                    lhsT_scale=en_scales[:, ns],
+                    rhs=h_codes[:, js].bitcast(FP8X4),
+                    rhs_scale=h_scales[:, js],
+                    start=True,
                     stop=True,
                 )
-            nc.scalar.activation(out=h_bf, in_=diff[:].rearrange("p t j -> p j t"), func=ACT.Abs)
-
-        def quantize_h(c, h_bf):
-            js = slice(JC * c, JC * (c + 1))
-            nc.vector.quantize_mx(
-                out=h_codes[:, js].bitcast(FP8X4),
-                scales=h_scales[:, js],
-                in_=h_bf.rearrange("p j t -> p (j t)"),
-            )
-
-        en_rows = en.rearrange("(p t) n -> p t n", t=PACK)
-        en_bf = rounded.tile([P, N, PACK], BF16, name="weight_bf", align_bytes=64)
-        en_codes = keep.tile([P, N], U32, align_bytes=64)
-        en_scales = keep.tile([P, N], U8, align_bytes=64)
-
-        def round_en(half):
-            en_raw = stage.tile([P, PACK, HALF], F32, name="stage", align_bytes=64)
-            nc.sync.dma_start(out=en_raw[:], in_=en_rows[:, :, HALF * half : HALF * (half + 1)])
-            on_scalar = P if half == 0 else 0
-            if on_scalar:
-                nc.scalar.copy(
-                    out=en_bf[:, 0:on_scalar, :].rearrange("p (c u) t -> p c t u", u=4),
-                    in_=en_raw[:, :, 0:on_scalar].rearrange("p t (c u) -> p c t u", u=4),
-                )
-            nc.vector.tensor_copy(
-                out=en_bf[:, HALF * half + on_scalar : HALF * (half + 1), :].rearrange("p (c u) t -> p c t u", u=4),
-                in_=en_raw[:, :, on_scalar:HALF].rearrange("p t (c u) -> p c t u", u=4),
-            )
-
-        def quantize_en(half):
-            ns = slice(HALF * half, HALF * (half + 1))
-            nc.vector.quantize_mx(
-                out=en_codes[:, ns].bitcast(FP8X4),
-                scales=en_scales[:, ns],
-                in_=en_bf[:, ns, :].rearrange("p n t -> p (n t)"),
-            )
-
-        def score(j_half, m, on_vector):
-            js = slice(HALF * j_half, HALF * (j_half + 1))
-            ns = slice(P * m, P * (m + 1))
-            y = psum.tile([P, HALF], F32, name="bank")
-            nc.tensor.matmul_mx(
-                out=y[:],
-                lhsT=en_codes[:, ns].bitcast(FP8X4),
-                lhsT_scale=en_scales[:, ns],
-                rhs=h_codes[:, js].bitcast(FP8X4),
-                rhs_scale=h_scales[:, js],
-                start=True,
-                stop=True,
-            )
-            staged = keep.tile([P, HALF], F32, name="staged_%d_%d" % (j_half, m))
-            if on_vector:
+            staged = keep.tile([P, count, width], F32, name="staged_%d_%d" % (j0, m0))
+            if engine == "vector":
                 nc.vector.tensor_copy(out=staged[:], in_=y[:])
             else:
                 nc.scalar.copy(out=staged[:], in_=y[:])
-            nc.sync.dma_start(out=out[ns, js], in_=staged[:])
+            rows = out[P * m0 : P * (m0 + count), js].rearrange("(m p) j -> p m j", p=P)
+            nc.sync.dma_start(out=rows, in_=staged[:])
 
-        round_en(0)
-        quantize_en(0)
-        round_en(1)
-        h_all = stage.tile([P, J, PACK], BF16, name="stage", align_bytes=64)
-        h_codes = stage.tile([P, J], U32, name="stage", align_bytes=64)
-        h_chunks = [h_all[:, JC * c : JC * (c + 1), :] for c in range(CHUNKS)]
-        for c in range(CHUNKS):
-            project(c, h_chunks[c])
-        quantize_h(0, h_chunks[0])
-        quantize_h(1, h_chunks[1])
-        quantize_en(1)
-        quantize_h(2, h_chunks[2])
-        score(0, 0, True)
-        quantize_h(3, h_chunks[3])
-        for m in range(1, 4):
-            score(0, m, m % 2 == 0)
-        for m in range(4):
-            score(1, m, m % 2 == 1)
+        rectify(0)
+        rectify(1)
+        rectify(2)
+        rectify(3)
+        nc.vector.tensor_copy(out=en_bf[0][:, 192 : 256, :].rearrange("p (c u) t -> p c t u", u=4), in_=en_raw[0][:, :, 192 : 256].rearrange("p t (c u) -> p c t u", u=4))
+        quantize_en(0, 256)
+        quantize_h(0, 128)
+        quantize_h(128, 256)
+        nc.vector.tensor_copy(out=en_bf[1][:, 0 : 256, :].rearrange("p (c u) t -> p c t u", u=4), in_=en_raw[1][:, :, 0 : 256].rearrange("p t (c u) -> p c t u", u=4))
+        quantize_en(256, 512)
+        quantize_h(256, 384)
+        quantize_h(384, 512)
+        score(0, 256, 0, 1, "vector")
+        score(0, 256, 1, 1, "scalar")
+        score(0, 256, 2, 1, "vector")
+        score(0, 256, 3, 1, "scalar")
+        score(256, 256, 0, 1, "vector")
+        score(256, 256, 1, 1, "scalar")
+        score(256, 256, 2, 1, "vector")
+        score(256, 256, 3, 1, "scalar")

@@ -28,6 +28,7 @@ def tile_list_kg_absd_none_kernel(tc, tab_words, tab_scales, tab2_words, tab2_sc
     with ExitStack() as ctx:
         keep = ctx.enter_context(tc.tile_pool(name="keep", bufs=1))
         reuse = ctx.enter_context(tc.tile_pool(name="reuse", bufs=1))
+        ring = ctx.enter_context(tc.tile_pool(name="ring", bufs=2))
         psum = ctx.enter_context(tc.psum_pool(name="psum", bufs=8))
 
         def load_scale_rows(engines, tile, scales):
@@ -37,7 +38,7 @@ def tile_list_kg_absd_none_kernel(tc, tab_words, tab_scales, tab2_words, tab2_sc
 
         list_a = keep.tile([P, J // 16], U16)
         list_b = keep.tile([P, J // 16], U16)
-        tab_a_scales = keep.tile([P, T // 4], I32, align_bytes=64)
+        tab_a_scales = reuse.tile([P, T // 4], I32, name="after_gathers", align_bytes=64)
         tab_b_scales = keep.tile([P, T // 4], I32, align_bytes=64)
         wb_scales_raw = keep.tile([P, R // 4], I32, align_bytes=64)
         tab_a_words = keep.tile([P, T], I32, align_bytes=64)
@@ -50,22 +51,24 @@ def tile_list_kg_absd_none_kernel(tc, tab_words, tab_scales, tab2_words, tab2_sc
 
         wa_rows = wa.rearrange("(p i) r -> p i r", i=PACK)
         en_rows = en.rearrange("(p t) n -> p t n", t=PACK)
-        wa_raw = [keep.tile([P, PACK, 512], F32, name="wa_raw_0")]
+        wa_raw = [keep.tile([P, PACK, 256], F32, name="wa_raw_0"), keep.tile([P, PACK, 256], F32, name="wa_raw_1")]
         en_raw = [keep.tile([P, PACK, 256], F32, name="en_raw_0"), keep.tile([P, PACK, 256], F32, name="en_raw_1")]
         nc.sync.dma_start(list_b[:], offs2)
         nc.sync.dma_start(out=wb_words_raw[:], in_=wb_words[0].bitcast(I32))
         load_scale_rows((nc.sync, nc.sync, nc.scalar, nc.scalar), tab_b_scales, tab2_scales)
         nc.sync.dma_start(out=tab_b_words[:], in_=tab2_words[0].rearrange("p t i -> p (t i)").bitcast(I32))
-        nc.sync.dma_start(out=tab_a_words[:], in_=tab_words[0].rearrange("p t i -> p (t i)").bitcast(I32))
+        nc.sync.dma_start(out=wa_raw[0][:], in_=wa_rows[:, :, 0 : 256])
         load_scale_rows((nc.sync, nc.sync, nc.sync, nc.sync), wb_scales_raw, wb_scales)
         nc.sync.dma_start(list_a[:], offs)
-        nc.sync.dma_start(out=wa_raw[0][:], in_=wa_rows[:, :, 0 : 512])
+        nc.sync.dma_start(out=wa_raw[1][:], in_=wa_rows[:, :, 256 : 512])
+        nc.sync.dma_start(out=tab_a_words[:], in_=tab_words[0].rearrange("p t i -> p (t i)").bitcast(I32))
         load_scale_rows((nc.sync, nc.sync, nc.sync, nc.sync), tab_a_scales, tab_scales)
         nc.sync.dma_start(out=en_raw[0][:], in_=en_rows[:, :, 0 : 256])
         nc.sync.dma_start(out=en_raw[1][:], in_=en_rows[:, :, 256 : 512])
 
         wa_bf = keep.tile([P, PACK, P, PACK], BF16, align_bytes=64)
-        nc.scalar.activation(out=wa_bf[:, :, 0 : 44, :].rearrange("p t m i -> p m i t"), in_=wa_raw[0][:, :, 0 : 176].rearrange("p i (m t) -> p m i t", t=PACK), func=ACT.Copy, scale=-1.0)
+        nc.scalar.activation(out=wa_bf[:, :, 0 : 64, :].rearrange("p t m i -> p m i t"), in_=wa_raw[0][:, :, 0 : 256].rearrange("p i (m t) -> p m i t", t=PACK), func=ACT.Copy, scale=-1.0)
+        nc.scalar.activation(out=wa_bf[:, :, 64 : 88, :].rearrange("p t m i -> p m i t"), in_=wa_raw[1][:, :, 0 : 96].rearrange("p i (m t) -> p m i t", t=PACK), func=ACT.Copy, scale=-1.0)
 
         b_scales = keep.tile([P, J], U8, align_bytes=64)
         b_words = keep.tile([P, J], U32, align_bytes=64)
@@ -103,38 +106,39 @@ def tile_list_kg_absd_none_kernel(tc, tab_words, tab_scales, tab2_words, tab2_sc
         a_scales = keep.tile([P, J], U8, align_bytes=64)
         wa_scales = keep.tile([P, R], U8, align_bytes=64)
         wa_codes = keep.tile([P, R], U32, align_bytes=64)
-        a_words = keep.tile([P, J], U32, align_bytes=64)
-        nc.vector.tensor_copy(a_words[:], tab_a_words[:].bitcast(U32).indirect(list_a[:, 0 : 32]))
-        nc.vector.tensor_scalar_mul(wa_bf[:, :, 44 : 128, :].rearrange("p t m i -> p m i t"), wa_raw[0][:, :, 176 : 512].rearrange("p i (m t) -> p m i t", t=PACK), -1.0)
+        nc.vector.tensor_scalar_mul(wa_bf[:, :, 88 : 128, :].rearrange("p t m i -> p m i t"), wa_raw[1][:, :, 96 : 256].rearrange("p i (m t) -> p m i t", t=PACK), -1.0)
         nc.vector.quantize_mx(out=wa_codes[:].bitcast(FP8X4), scales=wa_scales[:], in_=wa_bf[:].rearrange("p t m i -> p (t m i)"))
-        nc.vector.tensor_copy(a_scales[:, 0 : 128], tab_a_scales[:].bitcast(U8).indirect(list_a[:, 0 : 8]))
-        nc.vector.tensor_copy(a_scales[:, 128 : 256], tab_a_scales[:].bitcast(U8).indirect(list_a[:, 8 : 16]))
-        nc.vector.tensor_copy(a_scales[:, 256 : 384], tab_a_scales[:].bitcast(U8).indirect(list_a[:, 16 : 24]))
-        nc.vector.tensor_copy(a_scales[:, 384 : 512], tab_a_scales[:].bitcast(U8).indirect(list_a[:, 24 : 32]))
 
-        en_bf = [keep.tile([P, HALF, PACK], BF16, name="en_bf_%d" % half, align_bytes=64) for half in range(2)]
-        en_codes = keep.tile([P, N], U32, align_bytes=64)
+        en_bf = [
+            keep.tile([P, HALF, PACK], BF16, name="en_bf_0", align_bytes=64),
+            reuse.tile([P, HALF, PACK], BF16, name="after_gathers", align_bytes=64),
+        ]
+        en_codes = [keep.tile([P, HALF], U32, name="en_codes_0", align_bytes=64)]
         en_scales = keep.tile([P, N], U8, align_bytes=64)
-        nc.scalar.copy(out=en_bf[0][:, 0 : 192, :].rearrange("p (c u) t -> p c t u", u=4), in_=en_raw[0][:, :, 0 : 192].rearrange("p t (c u) -> p c t u", u=4))
+        nc.scalar.copy(out=en_bf[0][:, 0 : 256, :].rearrange("p (c u) t -> p c t u", u=4), in_=en_raw[0][:, :, 0 : 256].rearrange("p t (c u) -> p c t u", u=4))
 
-        h_bf = keep.tile([P, J, PACK], BF16, align_bytes=64)
+        h_bf = [(reuse if c == 1 else keep).tile([P, JC, PACK], BF16, name="h_bf_%d" % c, align_bytes=64) for c in range(CHUNKS)]
 
         def project_a(c):
             js = slice(JC * c, JC * (c + 1))
+            entries = list_a[:, JC * c // 16 : JC * (c + 1) // 16]
+            words = ring.tile([P, JC], U32, name="words", align_bytes=64)
+            nc.vector.tensor_copy(words[:], tab_a_words[:].bitcast(U32).indirect(entries))
+            nc.vector.tensor_copy(a_scales[:, js], tab_a_scales[:].bitcast(U8).indirect(entries))
             for t in range(PACK):
                 cols = slice(P * t, P * (t + 1))
                 nc.tensor.matmul_mx(
                     out=diff[c][:, t, :],
                     lhsT=wa_codes[:, cols].bitcast(FP8X4),
                     lhsT_scale=wa_scales[:, cols],
-                    rhs=a_words[:, js].bitcast(FP8X4),
+                    rhs=words[:].bitcast(FP8X4),
                     rhs_scale=a_scales[:, js],
                     start=False,
                     stop=(t == PACK - 1),
                 )
 
         def rectify(c):
-            nc.scalar.activation(out=h_bf[:, JC * c : JC * (c + 1), :], in_=diff[c][:].rearrange("p t j -> p j t"), func=ACT.Abs)
+            nc.scalar.activation(out=h_bf[c][:], in_=diff[c][:].rearrange("p t j -> p j t"), func=ACT.Abs)
 
         for c in range(CHUNKS):
             project_a(c)
@@ -146,13 +150,13 @@ def tile_list_kg_absd_none_kernel(tc, tab_words, tab_scales, tab2_words, tab2_sc
             nc.vector.quantize_mx(
                 out=h_codes[:, j0:j1].bitcast(FP8X4),
                 scales=h_scales[:, j0:j1],
-                in_=h_bf[:, j0:j1, :].rearrange("p j t -> p (j t)"),
+                in_=h_bf[j0 // JC][:].rearrange("p j t -> p (j t)"),
             )
 
         def quantize_en(n0, n1):
             half = n0 // HALF
             nc.vector.quantize_mx(
-                out=en_codes[:, n0:n1].bitcast(FP8X4),
+                out=en_codes[half][:, n0 - HALF * half : n1 - HALF * half].bitcast(FP8X4),
                 scales=en_scales[:, n0:n1],
                 in_=en_bf[half][:, n0 - HALF * half : n1 - HALF * half, :].rearrange("p n t -> p (n t)"),
             )
@@ -164,7 +168,7 @@ def tile_list_kg_absd_none_kernel(tc, tab_words, tab_scales, tab2_words, tab2_sc
                 ns = slice(P * (m0 + m), P * (m0 + m + 1))
                 nc.tensor.matmul_mx(
                     out=y[:, m, :],
-                    lhsT=en_codes[:, ns].bitcast(FP8X4),
+                    lhsT=en_codes[(m0 + m) // 2][:, P * ((m0 + m) % 2) : P * ((m0 + m) % 2 + 1)].bitcast(FP8X4),
                     lhsT_scale=en_scales[:, ns],
                     rhs=h_codes[:, js].bitcast(FP8X4),
                     rhs_scale=h_scales[:, js],
@@ -183,19 +187,19 @@ def tile_list_kg_absd_none_kernel(tc, tab_words, tab_scales, tab2_words, tab2_sc
         rectify(1)
         rectify(2)
         rectify(3)
-        nc.vector.tensor_copy(out=en_bf[0][:, 192 : 256, :].rearrange("p (c u) t -> p c t u", u=4), in_=en_raw[0][:, :, 192 : 256].rearrange("p t (c u) -> p c t u", u=4))
         quantize_en(0, 256)
+        nc.vector.tensor_copy(out=en_bf[1][:, 0 : 256, :].rearrange("p (c u) t -> p c t u", u=4), in_=en_raw[1][:, :, 0 : 256].rearrange("p t (c u) -> p c t u", u=4))
         quantize_h(0, 128)
         quantize_h(128, 256)
-        nc.vector.tensor_copy(out=en_bf[1][:, 0 : 256, :].rearrange("p (c u) t -> p c t u", u=4), in_=en_raw[1][:, :, 0 : 256].rearrange("p t (c u) -> p c t u", u=4))
+        en_codes.append(reuse.tile([P, HALF], U32, name="h_bf_1", align_bytes=64))
         quantize_en(256, 512)
         quantize_h(256, 384)
         quantize_h(384, 512)
-        score(0, 256, 0, 1, "vector")
-        score(0, 256, 1, 1, "scalar")
-        score(0, 256, 2, 1, "vector")
-        score(0, 256, 3, 1, "scalar")
-        score(256, 256, 0, 1, "vector")
-        score(256, 256, 1, 1, "scalar")
-        score(256, 256, 2, 1, "vector")
-        score(256, 256, 3, 1, "scalar")
+        score(0, 256, 0, 1, "scalar")
+        score(0, 256, 1, 1, "vector")
+        score(0, 256, 2, 1, "scalar")
+        score(0, 256, 3, 1, "vector")
+        score(256, 256, 0, 1, "scalar")
+        score(256, 256, 1, 1, "vector")
+        score(256, 256, 2, 1, "scalar")
+        score(256, 256, 3, 1, "vector")

@@ -28,7 +28,7 @@ def tile_list_kg_absd_none_kernel(tc, tab_words, tab_scales, tab2_words, tab2_sc
     with ExitStack() as ctx:
         keep = ctx.enter_context(tc.tile_pool(name="keep", bufs=1))
         reuse = ctx.enter_context(tc.tile_pool(name="reuse", bufs=1))
-        ring = ctx.enter_context(tc.tile_pool(name="ring", bufs=2))
+        area = ctx.enter_context(tc.tile_pool(name="area", bufs=1))
         psum = ctx.enter_context(tc.psum_pool(name="psum", bufs=8))
 
         def load_scale_rows(engines, tile, scales):
@@ -52,23 +52,23 @@ def tile_list_kg_absd_none_kernel(tc, tab_words, tab_scales, tab2_words, tab2_sc
         wa_rows = wa.rearrange("(p i) r -> p i r", i=PACK)
         en_rows = en.rearrange("(p t) n -> p t n", t=PACK)
         wa_raw = [keep.tile([P, PACK, 256], F32, name="wa_raw_0"), keep.tile([P, PACK, 256], F32, name="wa_raw_1")]
-        en_raw = [keep.tile([P, PACK, 256], F32, name="en_raw_0"), keep.tile([P, PACK, 256], F32, name="en_raw_1")]
+        en_raw = [area.tile([P, PACK, 256], F32, name="en_raw_0", align_bytes=64, offset=0), keep.tile([P, PACK, 256], F32, name="en_raw_1")]
         nc.sync.dma_start(list_b[:], offs2)
         nc.sync.dma_start(out=wb_words_raw[:], in_=wb_words[0].bitcast(I32))
         load_scale_rows((nc.sync, nc.sync, nc.scalar, nc.scalar), tab_b_scales, tab2_scales)
         nc.sync.dma_start(out=tab_b_words[:], in_=tab2_words[0].rearrange("p t i -> p (t i)").bitcast(I32))
-        nc.sync.dma_start(out=wa_raw[0][:], in_=wa_rows[:, :, 0 : 256])
+        nc.sync.dma_start(out=tab_a_words[:], in_=tab_words[0].rearrange("p t i -> p (t i)").bitcast(I32))
         load_scale_rows((nc.sync, nc.sync, nc.sync, nc.sync), wb_scales_raw, wb_scales)
         nc.sync.dma_start(list_a[:], offs)
+        nc.sync.dma_start(out=wa_raw[0][:], in_=wa_rows[:, :, 0 : 256])
         nc.sync.dma_start(out=wa_raw[1][:], in_=wa_rows[:, :, 256 : 512])
-        nc.sync.dma_start(out=tab_a_words[:], in_=tab_words[0].rearrange("p t i -> p (t i)").bitcast(I32))
         load_scale_rows((nc.sync, nc.sync, nc.sync, nc.sync), tab_a_scales, tab_scales)
         nc.sync.dma_start(out=en_raw[0][:], in_=en_rows[:, :, 0 : 256])
         nc.sync.dma_start(out=en_raw[1][:], in_=en_rows[:, :, 256 : 512])
 
-        wa_bf = keep.tile([P, PACK, P, PACK], BF16, align_bytes=64)
+        wa_bf = reuse.tile([P, PACK, P, PACK], BF16, name="weight", align_bytes=64)
         nc.scalar.activation(out=wa_bf[:, :, 0 : 64, :].rearrange("p t m i -> p m i t"), in_=wa_raw[0][:, :, 0 : 256].rearrange("p i (m t) -> p m i t", t=PACK), func=ACT.Copy, scale=-1.0)
-        nc.scalar.activation(out=wa_bf[:, :, 64 : 88, :].rearrange("p t m i -> p m i t"), in_=wa_raw[1][:, :, 0 : 96].rearrange("p i (m t) -> p m i t", t=PACK), func=ACT.Copy, scale=-1.0)
+        nc.scalar.activation(out=wa_bf[:, :, 64 : 112, :].rearrange("p t m i -> p m i t"), in_=wa_raw[1][:, :, 0 : 192].rearrange("p i (m t) -> p m i t", t=PACK), func=ACT.Copy, scale=-1.0)
 
         b_scales = keep.tile([P, J], U8, align_bytes=64)
         b_words = keep.tile([P, J], U32, align_bytes=64)
@@ -103,11 +103,19 @@ def tile_list_kg_absd_none_kernel(tc, tab_words, tab_scales, tab2_words, tab2_sc
         for c in range(CHUNKS):
             project_b(c)
 
-        a_scales = keep.tile([P, J], U8, align_bytes=64)
         wa_scales = keep.tile([P, R], U8, align_bytes=64)
         wa_codes = keep.tile([P, R], U32, align_bytes=64)
-        nc.vector.tensor_scalar_mul(wa_bf[:, :, 88 : 128, :].rearrange("p t m i -> p m i t"), wa_raw[1][:, :, 96 : 256].rearrange("p i (m t) -> p m i t", t=PACK), -1.0)
+        a_words = keep.tile([P, J], U32, align_bytes=64)
+        nc.vector.tensor_copy(a_words[:], tab_a_words[:].bitcast(U32).indirect(list_a[:, 0 : 32]))
+        nc.vector.tensor_scalar_mul(wa_bf[:, :, 112 : 128, :].rearrange("p t m i -> p m i t"), wa_raw[1][:, :, 192 : 256].rearrange("p i (m t) -> p m i t", t=PACK), -1.0)
         nc.vector.quantize_mx(out=wa_codes[:].bitcast(FP8X4), scales=wa_scales[:], in_=wa_bf[:].rearrange("p t m i -> p (t m i)"))
+        a_first = keep.tile([P, 256], U8, align_bytes=64)
+        a_rest = reuse.tile([P, J - 256], U8, name="weight", align_bytes=64)
+        a_scales = [a_first[:, JC * c : JC * (c + 1)] for c in range(2)] + [a_rest[:, JC * c : JC * (c + 1)] for c in range(2)]
+        nc.vector.tensor_copy(a_scales[0], tab_a_scales[:].bitcast(U8).indirect(list_a[:, 0 : 8]))
+        nc.vector.tensor_copy(a_scales[1], tab_a_scales[:].bitcast(U8).indirect(list_a[:, 8 : 16]))
+        nc.vector.tensor_copy(a_scales[2], tab_a_scales[:].bitcast(U8).indirect(list_a[:, 16 : 24]))
+        nc.vector.tensor_copy(a_scales[3], tab_a_scales[:].bitcast(U8).indirect(list_a[:, 24 : 32]))
 
         en_bf = [
             keep.tile([P, HALF, PACK], BF16, name="en_bf_0", align_bytes=64),
@@ -117,22 +125,18 @@ def tile_list_kg_absd_none_kernel(tc, tab_words, tab_scales, tab2_words, tab2_sc
         en_scales = keep.tile([P, N], U8, align_bytes=64)
         nc.scalar.copy(out=en_bf[0][:, 0 : 256, :].rearrange("p (c u) t -> p c t u", u=4), in_=en_raw[0][:, :, 0 : 256].rearrange("p t (c u) -> p c t u", u=4))
 
-        h_bf = [(reuse if c == 1 else keep).tile([P, JC, PACK], BF16, name="h_bf_%d" % c, align_bytes=64) for c in range(CHUNKS)]
+        h_bf = [area.tile([P, JC, PACK], BF16, name="h_bf_%d" % c, align_bytes=64, offset=1024 * c) for c in range(CHUNKS)]
 
         def project_a(c):
             js = slice(JC * c, JC * (c + 1))
-            entries = list_a[:, JC * c // 16 : JC * (c + 1) // 16]
-            words = ring.tile([P, JC], U32, name="words", align_bytes=64)
-            nc.vector.tensor_copy(words[:], tab_a_words[:].bitcast(U32).indirect(entries))
-            nc.vector.tensor_copy(a_scales[:, js], tab_a_scales[:].bitcast(U8).indirect(entries))
             for t in range(PACK):
                 cols = slice(P * t, P * (t + 1))
                 nc.tensor.matmul_mx(
                     out=diff[c][:, t, :],
                     lhsT=wa_codes[:, cols].bitcast(FP8X4),
                     lhsT_scale=wa_scales[:, cols],
-                    rhs=words[:].bitcast(FP8X4),
-                    rhs_scale=a_scales[:, js],
+                    rhs=a_words[:, js].bitcast(FP8X4),
+                    rhs_scale=a_scales[c],
                     start=False,
                     stop=(t == PACK - 1),
                 )
@@ -175,7 +179,10 @@ def tile_list_kg_absd_none_kernel(tc, tab_words, tab_scales, tab2_words, tab2_sc
                     start=True,
                     stop=True,
                 )
-            staged = keep.tile([P, count, width], F32, name="staged_%d_%d" % (j0, m0))
+            if (j0, m0) == (0, 2):
+                staged = area.tile([P, count, width], F32, name="staged_late", align_bytes=64, offset=3072)
+            else:
+                staged = keep.tile([P, count, width], F32, name="staged_%d_%d" % (j0, m0))
             if engine == "vector":
                 nc.vector.tensor_copy(out=staged[:], in_=y[:])
             else:
@@ -191,15 +198,15 @@ def tile_list_kg_absd_none_kernel(tc, tab_words, tab_scales, tab2_words, tab2_sc
         nc.vector.tensor_copy(out=en_bf[1][:, 0 : 256, :].rearrange("p (c u) t -> p c t u", u=4), in_=en_raw[1][:, :, 0 : 256].rearrange("p t (c u) -> p c t u", u=4))
         quantize_h(0, 128)
         quantize_h(128, 256)
-        en_codes.append(reuse.tile([P, HALF], U32, name="h_bf_1", align_bytes=64))
+        en_codes.append(area.tile([P, HALF], U32, name="en_codes_1", align_bytes=64, offset=1024 * 1))
         quantize_en(256, 512)
         quantize_h(256, 384)
         quantize_h(384, 512)
         score(0, 256, 0, 1, "scalar")
-        score(0, 256, 1, 1, "vector")
-        score(0, 256, 2, 1, "scalar")
-        score(0, 256, 3, 1, "vector")
-        score(256, 256, 0, 1, "scalar")
-        score(256, 256, 1, 1, "vector")
-        score(256, 256, 2, 1, "scalar")
-        score(256, 256, 3, 1, "vector")
+        score(0, 256, 1, 1, "scalar")
+        score(0, 256, 2, 1, "vector")
+        score(0, 256, 3, 1, "scalar")
+        score(256, 256, 0, 1, "vector")
+        score(256, 256, 1, 1, "scalar")
+        score(256, 256, 2, 1, "vector")
+        score(256, 256, 3, 1, "scalar")

@@ -51,7 +51,7 @@ def tile_list_kg_absd_none_kernel(tc, tab_words, tab_scales, tab2_words, tab2_sc
 
         wa_rows = wa.rearrange("(p i) r -> p i r", i=PACK)
         en_rows = en.rearrange("(p t) n -> p t n", t=PACK)
-        wa_raw = [keep.tile([P, PACK, 256], F32, name="wa_raw_0"), keep.tile([P, PACK, 256], F32, name="wa_raw_1")]
+        wa_raw = [keep.tile([P, PACK, 512], F32, name="wa_raw_0")]
         en_raw = [area.tile([P, PACK, 256], F32, name="en_raw_0", align_bytes=64, offset=0), keep.tile([P, PACK, 256], F32, name="en_raw_1")]
         nc.sync.dma_start(list_b[:], offs2)
         nc.sync.dma_start(out=wb_words_raw[:], in_=wb_words[0].bitcast(I32))
@@ -60,15 +60,13 @@ def tile_list_kg_absd_none_kernel(tc, tab_words, tab_scales, tab2_words, tab2_sc
         nc.sync.dma_start(out=tab_a_words[:], in_=tab_words[0].rearrange("p t i -> p (t i)").bitcast(I32))
         load_scale_rows((nc.sync, nc.sync, nc.sync, nc.sync), wb_scales_raw, wb_scales)
         nc.sync.dma_start(list_a[:], offs)
-        nc.sync.dma_start(out=wa_raw[0][:], in_=wa_rows[:, :, 0 : 256])
-        nc.sync.dma_start(out=wa_raw[1][:], in_=wa_rows[:, :, 256 : 512])
+        nc.sync.dma_start(out=wa_raw[0][:], in_=wa_rows[:, :, 0 : 512])
         load_scale_rows((nc.sync, nc.sync, nc.sync, nc.sync), tab_a_scales, tab_scales)
         nc.sync.dma_start(out=en_raw[0][:], in_=en_rows[:, :, 0 : 256])
         nc.sync.dma_start(out=en_raw[1][:], in_=en_rows[:, :, 256 : 512])
 
         wa_bf = reuse.tile([P, PACK, P, PACK], BF16, name="weight", align_bytes=64)
-        nc.scalar.activation(out=wa_bf[:, :, 0 : 64, :].rearrange("p t m i -> p m i t"), in_=wa_raw[0][:, :, 0 : 256].rearrange("p i (m t) -> p m i t", t=PACK), func=ACT.Copy, scale=-1.0)
-        nc.scalar.activation(out=wa_bf[:, :, 64 : 112, :].rearrange("p t m i -> p m i t"), in_=wa_raw[1][:, :, 0 : 192].rearrange("p i (m t) -> p m i t", t=PACK), func=ACT.Copy, scale=-1.0)
+        nc.scalar.activation(out=wa_bf[:, :, 0 : 44, :].rearrange("p t m i -> p m i t"), in_=wa_raw[0][:, :, 0 : 176].rearrange("p i (m t) -> p m i t", t=PACK), func=ACT.Copy, scale=-1.0)
 
         b_scales = keep.tile([P, J], U8, align_bytes=64)
         b_words = keep.tile([P, J], U32, align_bytes=64)
@@ -107,11 +105,11 @@ def tile_list_kg_absd_none_kernel(tc, tab_words, tab_scales, tab2_words, tab2_sc
         wa_codes = keep.tile([P, R], U32, align_bytes=64)
         a_words = keep.tile([P, J], U32, align_bytes=64)
         nc.vector.tensor_copy(a_words[:], tab_a_words[:].bitcast(U32).indirect(list_a[:, 0 : 32]))
-        nc.vector.tensor_scalar_mul(wa_bf[:, :, 112 : 128, :].rearrange("p t m i -> p m i t"), wa_raw[1][:, :, 192 : 256].rearrange("p i (m t) -> p m i t", t=PACK), -1.0)
+        nc.vector.tensor_scalar_mul(wa_bf[:, :, 44 : 128, :].rearrange("p t m i -> p m i t"), wa_raw[0][:, :, 176 : 512].rearrange("p i (m t) -> p m i t", t=PACK), -1.0)
         nc.vector.quantize_mx(out=wa_codes[:].bitcast(FP8X4), scales=wa_scales[:], in_=wa_bf[:].rearrange("p t m i -> p (t m i)"))
-        a_first = keep.tile([P, 256], U8, align_bytes=64)
-        a_rest = reuse.tile([P, J - 256], U8, name="weight", align_bytes=64)
-        a_scales = [a_first[:, JC * c : JC * (c + 1)] for c in range(2)] + [a_rest[:, JC * c : JC * (c + 1)] for c in range(2)]
+        a_first = keep.tile([P, 128], U8, align_bytes=64)
+        a_rest = reuse.tile([P, J - 128], U8, name="weight", align_bytes=64)
+        a_scales = [a_first[:, JC * c : JC * (c + 1)] for c in range(1)] + [a_rest[:, JC * c : JC * (c + 1)] for c in range(3)]
         nc.vector.tensor_copy(a_scales[0], tab_a_scales[:].bitcast(U8).indirect(list_a[:, 0 : 8]))
         nc.vector.tensor_copy(a_scales[1], tab_a_scales[:].bitcast(U8).indirect(list_a[:, 8 : 16]))
         nc.vector.tensor_copy(a_scales[2], tab_a_scales[:].bitcast(U8).indirect(list_a[:, 16 : 24]))

@@ -106,11 +106,18 @@ def tile_list_kg_absd_none_kernel(tc, tab_words, tab_scales, tab2_words, tab2_sc
         a_words = keep.tile([P, J], U32, align_bytes=64)
         nc.vector.tensor_copy(a_words[:], tab_a_words[:].bitcast(U32).indirect(list_a[:, 0 : 32]))
         nc.vector.tensor_scalar_mul(wa_bf[:, :, 44 : 128, :].rearrange("p t m i -> p m i t"), wa_raw[0][:, :, 176 : 512].rearrange("p i (m t) -> p m i t", t=PACK), -1.0)
-        nc.vector.quantize_mx(out=wa_codes[:].bitcast(FP8X4), scales=wa_scales[:], in_=wa_bf[:].rearrange("p t m i -> p (t m i)"))
         a_first = keep.tile([P, 128], U8, align_bytes=64)
-        a_rest = reuse.tile([P, J - 128], U8, name="weight", align_bytes=64)
-        a_scales = [a_first[:, JC * c : JC * (c + 1)] for c in range(1)] + [a_rest[:, JC * c : JC * (c + 1)] for c in range(3)]
+        a_scales = [a_first[:, JC * c : JC * (c + 1)] for c in range(1)]
         nc.vector.tensor_copy(a_scales[0], tab_a_scales[:].bitcast(U8).indirect(list_a[:, 0 : 8]))
+        for t in (0, 2):
+            cols = slice(P * t, P * (t + 2))
+            nc.vector.quantize_mx(
+                out=wa_codes[:, cols].bitcast(FP8X4),
+                scales=wa_scales[:, cols],
+                in_=wa_bf[:, t : t + 2, :, :].rearrange("p t m i -> p (t m i)"),
+            )
+        a_rest = reuse.tile([P, J - 128], U8, name="weight", align_bytes=64)
+        a_scales.extend(a_rest[:, JC * c : JC * (c + 1)] for c in range(3))
         nc.vector.tensor_copy(a_scales[1], tab_a_scales[:].bitcast(U8).indirect(list_a[:, 8 : 16]))
         nc.vector.tensor_copy(a_scales[2], tab_a_scales[:].bitcast(U8).indirect(list_a[:, 16 : 24]))
         nc.vector.tensor_copy(a_scales[3], tab_a_scales[:].bitcast(U8).indirect(list_a[:, 24 : 32]))
@@ -181,12 +188,13 @@ def tile_list_kg_absd_none_kernel(tc, tab_words, tab_scales, tab2_words, tab2_sc
                 staged = area.tile([P, count, width], F32, name="staged_late", align_bytes=64, offset=3072)
             else:
                 staged = keep.tile([P, count, width], F32, name="staged_%d_%d" % (j0, m0))
+            rows = out[P * m0 : P * (m0 + count), js].rearrange("(m p) j -> p m j", p=P)
             if engine == "vector":
                 nc.vector.tensor_copy(out=staged[:], in_=y[:])
+                nc.sync.dma_start(out=rows, in_=staged[:])
             else:
                 nc.scalar.copy(out=staged[:], in_=y[:])
-            rows = out[P * m0 : P * (m0 + count), js].rearrange("(m p) j -> p m j", p=P)
-            nc.sync.dma_start(out=rows, in_=staged[:])
+                nc.scalar.dma_start(out=rows, in_=staged[:])
 
         rectify(0)
         rectify(1)

@@ -20,14 +20,13 @@ PACK = 4
 JC = 128
 CHUNKS = J // JC
 HALF = 256
-MH = HALF // PACK
+WA_SCALAR_END = 84
 
 
 def tile_list_kg_absd_none_kernel(tc, tab_words, tab_scales, tab2_words, tab2_scales, wa, wb_words, wb_scales, en, offs, offs2, out):
     nc = tc.nc
     with ExitStack() as ctx:
         keep = ctx.enter_context(tc.tile_pool(name="keep", bufs=1))
-        reuse = ctx.enter_context(tc.tile_pool(name="reuse", bufs=1))
         area = ctx.enter_context(tc.tile_pool(name="area", bufs=1))
         psum = ctx.enter_context(tc.psum_pool(name="psum", bufs=8))
 
@@ -38,7 +37,7 @@ def tile_list_kg_absd_none_kernel(tc, tab_words, tab_scales, tab2_words, tab2_sc
 
         list_a = keep.tile([P, J // 16], U16)
         list_b = keep.tile([P, J // 16], U16)
-        tab_a_scales = reuse.tile([P, T // 4], I32, name="after_gathers", align_bytes=64)
+        tab_a_scales = keep.tile([P, T // 4], I32, align_bytes=64)
         tab_b_scales = keep.tile([P, T // 4], I32, align_bytes=64)
         wb_scales_raw = keep.tile([P, R // 4], I32, align_bytes=64)
         tab_a_words = keep.tile([P, T], I32, align_bytes=64)
@@ -51,22 +50,32 @@ def tile_list_kg_absd_none_kernel(tc, tab_words, tab_scales, tab2_words, tab2_sc
 
         wa_rows = wa.rearrange("(p i) r -> p i r", i=PACK)
         en_rows = en.rearrange("(p t) n -> p t n", t=PACK)
-        wa_raw = [keep.tile([P, PACK, 512], F32, name="wa_raw_0")]
-        en_raw = [area.tile([P, PACK, 256], F32, name="en_raw_0", align_bytes=64, offset=0), keep.tile([P, PACK, 256], F32, name="en_raw_1")]
+        wa_raw = [keep.tile([P, PACK, HALF], F32, name="wa_raw_%d" % h) for h in range(2)]
+        en_raw = [keep.tile([P, PACK, HALF], F32, name="en_raw_%d" % h) for h in range(2)]
+        sync4 = (nc.sync, nc.sync, nc.sync, nc.sync)
         nc.sync.dma_start(list_b[:], offs2)
         nc.sync.dma_start(out=wb_words_raw[:], in_=wb_words[0].bitcast(I32))
         load_scale_rows((nc.sync, nc.sync, nc.scalar, nc.scalar), tab_b_scales, tab2_scales)
         nc.sync.dma_start(out=tab_b_words[:], in_=tab2_words[0].rearrange("p t i -> p (t i)").bitcast(I32))
-        nc.sync.dma_start(out=tab_a_words[:], in_=tab_words[0].rearrange("p t i -> p (t i)").bitcast(I32))
-        load_scale_rows((nc.sync, nc.sync, nc.sync, nc.sync), wb_scales_raw, wb_scales)
+        nc.sync.dma_start(out=wa_raw[0][:], in_=wa_rows[:, :, 0:HALF])
+        load_scale_rows(sync4, wb_scales_raw, wb_scales)
         nc.sync.dma_start(list_a[:], offs)
-        nc.sync.dma_start(out=wa_raw[0][:], in_=wa_rows[:, :, 0 : 512])
-        load_scale_rows((nc.sync, nc.sync, nc.sync, nc.sync), tab_a_scales, tab_scales)
-        nc.sync.dma_start(out=en_raw[0][:], in_=en_rows[:, :, 0 : 256])
-        nc.sync.dma_start(out=en_raw[1][:], in_=en_rows[:, :, 256 : 512])
+        nc.sync.dma_start(out=wa_raw[1][:], in_=wa_rows[:, :, HALF:R])
+        nc.sync.dma_start(out=en_raw[0][:], in_=en_rows[:, :, 0:HALF])
+        load_scale_rows(sync4, tab_a_scales, tab_scales)
+        nc.sync.dma_start(out=tab_a_words[:], in_=tab_words[0].rearrange("p t i -> p (t i)").bitcast(I32))
+        nc.sync.dma_start(out=en_raw[1][:], in_=en_rows[:, :, HALF:N])
 
-        wa_bf = reuse.tile([P, PACK, P, PACK], BF16, name="weight", align_bytes=64)
-        nc.scalar.activation(out=wa_bf[:, :, 0 : 44, :].rearrange("p t m i -> p m i t"), in_=wa_raw[0][:, :, 0 : 176].rearrange("p i (m t) -> p m i t", t=PACK), func=ACT.Copy, scale=-1.0)
+        wa_bf = keep.tile([P, PACK, P, PACK], BF16, align_bytes=64)
+
+        def wa_views(m0, m1):
+            half = m0 // 64
+            src = wa_raw[half][:, :, PACK * m0 - HALF * half : PACK * m1 - HALF * half].rearrange("p i (m t) -> p m i t", t=PACK)
+            return wa_bf[:, :, m0:m1, :].rearrange("p t m i -> p m i t"), src
+
+        for m0, m1 in ((0, 64), (64, WA_SCALAR_END)):
+            dst, src = wa_views(m0, m1)
+            nc.scalar.activation(out=dst, in_=src, func=ACT.Copy, scale=-1.0)
 
         b_scales = keep.tile([P, J], U8, align_bytes=64)
         b_words = keep.tile([P, J], U32, align_bytes=64)
@@ -85,7 +94,7 @@ def tile_list_kg_absd_none_kernel(tc, tab_words, tab_scales, tab2_words, tab2_sc
 
         diff = [psum.tile([P, PACK, JC], F32, name="bank") for c in range(CHUNKS)]
 
-        def project_b(c):
+        for c in range(CHUNKS):
             js = slice(JC * c, JC * (c + 1))
             for t in range(PACK):
                 nc.tensor.matmul_mx(
@@ -98,121 +107,98 @@ def tile_list_kg_absd_none_kernel(tc, tab_words, tab_scales, tab2_words, tab2_sc
                     stop=False,
                 )
 
-        for c in range(CHUNKS):
-            project_b(c)
-
         wa_scales = keep.tile([P, R], U8, align_bytes=64)
         wa_codes = keep.tile([P, R], U32, align_bytes=64)
-        a_words = keep.tile([P, J], U32, align_bytes=64)
-        nc.vector.tensor_copy(a_words[:], tab_a_words[:].bitcast(U32).indirect(list_a[:, 0 : 32]))
-        nc.vector.tensor_scalar_mul(wa_bf[:, :, 44 : 128, :].rearrange("p t m i -> p m i t"), wa_raw[0][:, :, 176 : 512].rearrange("p i (m t) -> p m i t", t=PACK), -1.0)
-        a_first = keep.tile([P, 128], U8, align_bytes=64)
-        a_scales = [a_first[:, JC * c : JC * (c + 1)] for c in range(1)]
-        nc.vector.tensor_copy(a_scales[0], tab_a_scales[:].bitcast(U8).indirect(list_a[:, 0 : 8]))
-        for t in (0, 2):
-            cols = slice(P * t, P * (t + 2))
-            nc.vector.quantize_mx(
-                out=wa_codes[:, cols].bitcast(FP8X4),
-                scales=wa_scales[:, cols],
-                in_=wa_bf[:, t : t + 2, :, :].rearrange("p t m i -> p (t m i)"),
-            )
-        a_rest = reuse.tile([P, J - 128], U8, name="weight", align_bytes=64)
-        a_scales.extend(a_rest[:, JC * c : JC * (c + 1)] for c in range(3))
-        nc.vector.tensor_copy(a_scales[1], tab_a_scales[:].bitcast(U8).indirect(list_a[:, 8 : 16]))
-        nc.vector.tensor_copy(a_scales[2], tab_a_scales[:].bitcast(U8).indirect(list_a[:, 16 : 24]))
-        nc.vector.tensor_copy(a_scales[3], tab_a_scales[:].bitcast(U8).indirect(list_a[:, 24 : 32]))
+        dst, src = wa_views(WA_SCALAR_END, P)
+        nc.vector.tensor_scalar_mul(dst, src, -1.0)
+        nc.vector.quantize_mx(out=wa_codes[:].bitcast(FP8X4), scales=wa_scales[:], in_=wa_bf[:].rearrange("p t m i -> p (t m i)"))
+        a_early = keep.tile([P, 3 * JC], U8, align_bytes=64)
+        nc.vector.tensor_copy(a_early[:], tab_a_scales[:].bitcast(U8).indirect(list_a[:, 0:24]))
+        a_words = [area.tile([P, JC], U32, name="a_words_0", align_bytes=64, offset=0)]
+        a_words.extend(keep.tile([P, JC], U32, name="a_words_%d" % c, align_bytes=64) for c in range(1, CHUNKS))
+        for c in range(CHUNKS):
+            nc.vector.tensor_copy(a_words[c][:], tab_a_words[:].bitcast(U32).indirect(list_a[:, 8 * c : 8 * (c + 1)]))
 
-        en_bf = [
-            keep.tile([P, HALF, PACK], BF16, name="en_bf_0", align_bytes=64),
-            reuse.tile([P, HALF, PACK], BF16, name="after_gathers", align_bytes=64),
-        ]
-        en_codes = [keep.tile([P, HALF], U32, name="en_codes_0", align_bytes=64)]
-        en_scales = keep.tile([P, N], U8, align_bytes=64)
-        nc.scalar.copy(out=en_bf[0][:, 0 : 256, :].rearrange("p (c u) t -> p c t u", u=4), in_=en_raw[0][:, :, 0 : 256].rearrange("p t (c u) -> p c t u", u=4))
+        en_bf = [keep.tile([P, HALF, PACK], BF16, name="en_bf_%d" % h, align_bytes=64) for h in range(2)]
+        nc.scalar.copy(out=en_bf[0][:].rearrange("p (c u) t -> p c t u", u=4), in_=en_raw[0][:].rearrange("p t (c u) -> p c t u", u=4))
 
-        h_bf = [area.tile([P, JC, PACK], BF16, name="h_bf_%d" % c, align_bytes=64, offset=1024 * c) for c in range(CHUNKS)]
+        h_bf = [keep.tile([P, JC, PACK], BF16, name="h_bf_%d" % c, align_bytes=64) for c in range(CHUNKS)]
 
-        def project_a(c):
-            js = slice(JC * c, JC * (c + 1))
+        def project_a(c, scales):
             for t in range(PACK):
                 cols = slice(P * t, P * (t + 1))
                 nc.tensor.matmul_mx(
                     out=diff[c][:, t, :],
                     lhsT=wa_codes[:, cols].bitcast(FP8X4),
                     lhsT_scale=wa_scales[:, cols],
-                    rhs=a_words[:, js].bitcast(FP8X4),
-                    rhs_scale=a_scales[c],
+                    rhs=a_words[c][:].bitcast(FP8X4),
+                    rhs_scale=scales,
                     start=False,
                     stop=(t == PACK - 1),
                 )
 
-        def rectify(c):
+        for c in range(CHUNKS - 1):
+            project_a(c, a_early[:, JC * c : JC * (c + 1)])
+        a_late = area.tile([P, JC], U8, name="a_late", align_bytes=64, offset=0)
+        nc.vector.tensor_copy(a_late[:], tab_a_scales[:].bitcast(U8).indirect(list_a[:, 24:32]))
+        project_a(CHUNKS - 1, a_late[:])
+        for c in range(CHUNKS):
             nc.scalar.activation(out=h_bf[c][:], in_=diff[c][:].rearrange("p t j -> p j t"), func=ACT.Abs)
 
-        for c in range(CHUNKS):
-            project_a(c)
-
+        en_codes = [keep.tile([P, HALF], U32, name="en_codes_%d" % h, align_bytes=64) for h in range(2)]
+        en_scales = [
+            area.tile([P, HALF], U8, name="en_scales_0", align_bytes=64, offset=128),
+            keep.tile([P, HALF], U8, name="en_scales_1", align_bytes=64),
+        ]
         h_codes = keep.tile([P, J], U32, align_bytes=64)
         h_scales = keep.tile([P, J], U8, align_bytes=64)
 
-        def quantize_h(j0, j1):
-            nc.vector.quantize_mx(
-                out=h_codes[:, j0:j1].bitcast(FP8X4),
-                scales=h_scales[:, j0:j1],
-                in_=h_bf[j0 // JC][:].rearrange("p j t -> p (j t)"),
-            )
+        def quantize_h(c):
+            js = slice(JC * c, JC * (c + 1))
+            nc.vector.quantize_mx(out=h_codes[:, js].bitcast(FP8X4), scales=h_scales[:, js], in_=h_bf[c][:].rearrange("p j t -> p (j t)"))
 
-        def quantize_en(n0, n1):
-            half = n0 // HALF
-            nc.vector.quantize_mx(
-                out=en_codes[half][:, n0 - HALF * half : n1 - HALF * half].bitcast(FP8X4),
-                scales=en_scales[:, n0:n1],
-                in_=en_bf[half][:, n0 - HALF * half : n1 - HALF * half, :].rearrange("p n t -> p (n t)"),
-            )
+        def quantize_en(half):
+            nc.vector.quantize_mx(out=en_codes[half][:].bitcast(FP8X4), scales=en_scales[half][:], in_=en_bf[half][:].rearrange("p n t -> p (n t)"))
 
-        def score(j0, width, m0, count, engine):
-            js = slice(j0, j0 + width)
-            y = psum.tile([P, count, width], F32, name="bank")
-            for m in range(count):
-                ns = slice(P * (m0 + m), P * (m0 + m + 1))
-                nc.tensor.matmul_mx(
-                    out=y[:, m, :],
-                    lhsT=en_codes[(m0 + m) // 2][:, P * ((m0 + m) % 2) : P * ((m0 + m) % 2 + 1)].bitcast(FP8X4),
-                    lhsT_scale=en_scales[:, ns],
-                    rhs=h_codes[:, js].bitcast(FP8X4),
-                    rhs_scale=h_scales[:, js],
-                    start=True,
-                    stop=True,
-                )
-            if (j0, m0) == (0, 2):
-                staged = area.tile([P, count, width], F32, name="staged_late", align_bytes=64, offset=3072)
-            else:
-                staged = keep.tile([P, count, width], F32, name="staged_%d_%d" % (j0, m0))
-            rows = out[P * m0 : P * (m0 + count), js].rearrange("(m p) j -> p m j", p=P)
+        def score(j0, m, engine):
+            js = slice(j0, j0 + HALF)
+            ns = slice(P * (m % 2), P * (m % 2 + 1))
+            y = psum.tile([P, HALF], F32, name="bank")
+            nc.tensor.matmul_mx(
+                out=y[:],
+                lhsT=en_codes[m // 2][:, ns].bitcast(FP8X4),
+                lhsT_scale=en_scales[m // 2][:, ns],
+                rhs=h_codes[:, js].bitcast(FP8X4),
+                rhs_scale=h_scales[:, js],
+                start=True,
+                stop=True,
+            )
+            staged = keep.tile([P, HALF], F32, name="staged_%d_%d" % (j0, m))
             if engine == "vector":
                 nc.vector.tensor_copy(out=staged[:], in_=y[:])
-                nc.sync.dma_start(out=rows, in_=staged[:])
             else:
                 nc.scalar.copy(out=staged[:], in_=y[:])
-                nc.scalar.dma_start(out=rows, in_=staged[:])
+            nc.sync.dma_start(out=out[P * m : P * (m + 1), js], in_=staged[:])
 
-        rectify(0)
-        rectify(1)
-        rectify(2)
-        rectify(3)
-        quantize_en(0, 256)
-        nc.vector.tensor_copy(out=en_bf[1][:, 0 : 256, :].rearrange("p (c u) t -> p c t u", u=4), in_=en_raw[1][:, :, 0 : 256].rearrange("p t (c u) -> p c t u", u=4))
-        quantize_h(0, 128)
-        quantize_h(128, 256)
-        en_codes.append(area.tile([P, HALF], U32, name="en_codes_1", align_bytes=64, offset=1024 * 1))
-        quantize_en(256, 512)
-        quantize_h(256, 384)
-        quantize_h(384, 512)
-        score(0, 256, 0, 1, "scalar")
-        score(0, 256, 1, 1, "scalar")
-        score(0, 256, 2, 1, "vector")
-        score(0, 256, 3, 1, "scalar")
-        score(256, 256, 0, 1, "vector")
-        score(256, 256, 1, 1, "scalar")
-        score(256, 256, 2, 1, "vector")
-        score(256, 256, 3, 1, "scalar")
+        def round_en(n0, n1):
+            nc.vector.tensor_copy(
+                out=en_bf[1][:, n0:n1, :].rearrange("p (c u) t -> p c t u", u=4),
+                in_=en_raw[1][:, :, n0:n1].rearrange("p t (c u) -> p c t u", u=4),
+            )
+
+        quantize_en(0)
+        quantize_h(0)
+        quantize_h(1)
+        round_en(0, P)
+        round_en(P, HALF)
+        score(0, 0, "vector")
+        quantize_en(1)
+        quantize_h(2)
+        quantize_h(3)
+        score(0, 1, "scalar")
+        score(0, 2, "scalar")
+        score(0, 3, "scalar")
+        score(HALF, 0, "vector")
+        score(HALF, 1, "vector")
+        score(HALF, 2, "scalar")
+        score(HALF, 3, "vector")

@@ -29,176 +29,243 @@ def tile_list_kg_absd_none_kernel(tc, tab_words, tab_scales, tab2_words, tab2_sc
         keep = ctx.enter_context(tc.tile_pool(name="keep", bufs=1))
         area = ctx.enter_context(tc.tile_pool(name="area", bufs=1))
         psum = ctx.enter_context(tc.psum_pool(name="psum", bufs=8))
+        placed = {"a_words_0": 0, "a_scales_3": 0, "en_scales_0": 128, "h_bf_3": 1024, "staged_0_2": 1024}
+
+        def sbuf(name, shape, dtype):
+            if name in placed:
+                return area.tile(shape, dtype, name=name, align_bytes=64, offset=placed[name])
+            return keep.tile(shape, dtype, name=name, align_bytes=64)
 
         def load_scale_rows(engines, tile, scales):
             rows = scales[0].bitcast(I32)
             for quad in range(4):
                 engines[quad].dma_start(out=tile[32 * quad : 32 * quad + 4, :], in_=rows[4 * quad : 4 * quad + 4, :])
 
-        list_a = keep.tile([P, J // 16], U16)
-        list_b = keep.tile([P, J // 16], U16)
-        tab_a_scales = keep.tile([P, T // 4], I32, align_bytes=64)
-        tab_b_scales = keep.tile([P, T // 4], I32, align_bytes=64)
-        wb_scales_raw = keep.tile([P, R // 4], I32, align_bytes=64)
-        tab_a_words = keep.tile([P, T], I32, align_bytes=64)
-        tab_b_words = keep.tile([P, T], I32, align_bytes=64)
-        wb_words_raw = keep.tile([P, R // 2], I32, align_bytes=64)
-
-        nc.vector.memset(tab_b_scales[:], 0)
-        nc.vector.memset(wb_scales_raw[:], 0)
-        nc.vector.memset(tab_a_scales[:], 0)
-
+        list_a = keep.tile([P, J // 16], U16, name="list_a")
+        list_b = keep.tile([P, J // 16], U16, name="list_b")
+        tab_a_scales = sbuf("tab_a_scales", [P, T // 4], I32)
+        tab_b_scales = sbuf("tab_b_scales", [P, T // 4], I32)
+        wb_scales_raw = sbuf("wb_scales_raw", [P, R // 4], I32)
+        tab_a_words = sbuf("tab_a_words", [P, T], I32)
+        tab_b_words = sbuf("tab_b_words", [P, T], I32)
+        wb_words_raw = sbuf("wb_words_raw", [P, R // 2], I32)
         wa_rows = wa.rearrange("(p i) r -> p i r", i=PACK)
         en_rows = en.rearrange("(p t) n -> p t n", t=PACK)
-        wa_raw = [keep.tile([P, PACK, HALF], F32, name="wa_raw_%d" % h) for h in range(2)]
-        en_raw = [keep.tile([P, PACK, HALF], F32, name="en_raw_%d" % h) for h in range(2)]
+        wa_raw = [sbuf("wa_raw_%d" % h, [P, PACK, HALF], F32) for h in range(2)]
+        en_raw = [sbuf("en_raw_%d" % h, [P, PACK, HALF], F32) for h in range(2)]
         sync4 = (nc.sync, nc.sync, nc.sync, nc.sync)
-        nc.sync.dma_start(list_b[:], offs2)
-        nc.sync.dma_start(out=wb_words_raw[:], in_=wb_words[0].bitcast(I32))
-        load_scale_rows((nc.sync, nc.sync, nc.scalar, nc.scalar), tab_b_scales, tab2_scales)
-        nc.sync.dma_start(out=tab_b_words[:], in_=tab2_words[0].rearrange("p t i -> p (t i)").bitcast(I32))
-        nc.sync.dma_start(out=wa_raw[0][:], in_=wa_rows[:, :, 0:HALF])
-        load_scale_rows(sync4, wb_scales_raw, wb_scales)
-        nc.sync.dma_start(list_a[:], offs)
-        nc.sync.dma_start(out=wa_raw[1][:], in_=wa_rows[:, :, HALF:R])
-        nc.sync.dma_start(out=en_raw[0][:], in_=en_rows[:, :, 0:HALF])
-        load_scale_rows(sync4, tab_a_scales, tab_scales)
-        nc.sync.dma_start(out=tab_a_words[:], in_=tab_words[0].rearrange("p t i -> p (t i)").bitcast(I32))
-        nc.sync.dma_start(out=en_raw[1][:], in_=en_rows[:, :, HALF:N])
+        mixed4 = (nc.sync, nc.sync, nc.scalar, nc.scalar)
+        scalar4 = (nc.scalar, nc.scalar, nc.scalar, nc.scalar)
+        made = {}
 
-        wa_bf = keep.tile([P, PACK, P, PACK], BF16, align_bytes=64)
+        def once(name, shape, dtype):
+            if name not in made:
+                made.update({name: sbuf(name, shape, dtype)})
+            return made[name]
 
-        def wa_views(m0, m1):
+        def load_words(tile, words):
+            nc.sync.dma_start(out=tile[:], in_=words[0].rearrange("p t i -> p (t i)").bitcast(I32))
+
+        def load_half(tiles, rows, h):
+            nc.sync.dma_start(out=tiles[h][:], in_=rows[:, :, HALF * h : HALF * (h + 1)])
+
+        def round_wa(engine, m0, m1):
             half = m0 // 64
-            src = wa_raw[half][:, :, PACK * m0 - HALF * half : PACK * m1 - HALF * half].rearrange("p i (m t) -> p m i t", t=PACK)
-            return wa_bf[:, :, m0:m1, :].rearrange("p t m i -> p m i t"), src
+            src = wa_raw[half][:, :, PACK * m0 - HALF * half : PACK * m1 - HALF * half].rearrange("p i (m t) -> p m t i", t=PACK)
+            dst = once("wa_bf", [P, PACK, P, PACK], BF16)[:, :, m0:m1, :].rearrange("p t m i -> p m t i")
+            if engine == "scalar":
+                nc.scalar.activation(out=dst, in_=src, func=ACT.Copy, scale=-1.0)
+            else:
+                nc.vector.tensor_scalar_mul(dst, src, -1.0)
 
-        for m0, m1 in ((0, 64), (64, WA_SCALAR_END)):
-            dst, src = wa_views(m0, m1)
-            nc.scalar.activation(out=dst, in_=src, func=ACT.Copy, scale=-1.0)
+        def deal_wb_words():
+            nc.vector.tensor_copy(
+                out=once("wb_codes", [P, 2 * R], U8)[:].bitcast(U16).rearrange("p (t m) -> p t m", t=PACK),
+                in_=wb_words_raw[:].bitcast(U16).rearrange("p (m t) -> p t m", t=PACK),
+            )
 
-        b_scales = keep.tile([P, J], U8, align_bytes=64)
-        b_words = keep.tile([P, J], U32, align_bytes=64)
-        wb_codes = keep.tile([P, 2 * R], U8, align_bytes=64)
-        wb_plane = keep.tile([P, R], U8, align_bytes=64)
-        nc.vector.tensor_copy(
-            out=wb_codes[:].bitcast(U16).rearrange("p (t m) -> p t m", t=PACK),
-            in_=wb_words_raw[:].bitcast(U16).rearrange("p (m t) -> p t m", t=PACK),
-        )
-        nc.vector.tensor_copy(b_scales[:], tab_b_scales[:].bitcast(U8).indirect(list_b[:]))
-        nc.vector.tensor_copy(b_words[:], tab_b_words[:].bitcast(U32).indirect(list_b[:]))
-        nc.vector.tensor_copy(
-            out=wb_plane[:].rearrange("p (t m) -> p m t", t=PACK),
-            in_=wb_scales_raw[:].bitcast(U8).rearrange("p (m t) -> p m t", t=PACK),
-        )
+        def deal_wb_scales():
+            nc.vector.tensor_copy(
+                out=once("wb_plane", [P, R], U8)[:].rearrange("p (t m) -> p m t", t=PACK),
+                in_=wb_scales_raw[:].bitcast(U8).rearrange("p (m t) -> p m t", t=PACK),
+            )
+
+        picked = {}
+
+        def gather(kind, c0, c1):
+            window, offsets, dtype = {
+                "a_words": (tab_a_words, list_a, U32),
+                "a_scales": (tab_a_scales, list_a, U8),
+                "b_words": (tab_b_words, list_b, U32),
+                "b_scales": (tab_b_scales, list_b, U8),
+            }[kind]
+            tile = sbuf("%s_%d" % (kind, c0), [P, JC * (c1 - c0)], dtype)
+            nc.vector.tensor_copy(tile[:], window[:].bitcast(dtype).indirect(offsets[:, 8 * c0 : 8 * c1]))
+            for c in range(c0, c1):
+                picked.update({(kind, c): tile[:, JC * (c - c0) : JC * (c - c0 + 1)]})
 
         diff = [psum.tile([P, PACK, JC], F32, name="bank") for c in range(CHUNKS)]
 
-        for c in range(CHUNKS):
-            js = slice(JC * c, JC * (c + 1))
+        def project_b(c):
             for t in range(PACK):
                 nc.tensor.matmul_mx(
                     out=diff[c][:, t, :],
-                    lhsT=wb_codes[:, 2 * P * t : 2 * P * (t + 1)].bitcast(FP4X4),
-                    lhsT_scale=wb_plane[:, P * t : P * (t + 1)],
-                    rhs=b_words[:, js].bitcast(FP8X4),
-                    rhs_scale=b_scales[:, js],
+                    lhsT=made["wb_codes"][:, 2 * P * t : 2 * P * (t + 1)].bitcast(FP4X4),
+                    lhsT_scale=made["wb_plane"][:, P * t : P * (t + 1)],
+                    rhs=picked[("b_words", c)].bitcast(FP8X4),
+                    rhs_scale=picked[("b_scales", c)],
                     start=(t == 0),
                     stop=False,
                 )
 
-        wa_scales = keep.tile([P, R], U8, align_bytes=64)
-        wa_codes = keep.tile([P, R], U32, align_bytes=64)
-        dst, src = wa_views(WA_SCALAR_END, P)
-        nc.vector.tensor_scalar_mul(dst, src, -1.0)
-        nc.vector.quantize_mx(out=wa_codes[:].bitcast(FP8X4), scales=wa_scales[:], in_=wa_bf[:].rearrange("p t m i -> p (t m i)"))
-        a_early = keep.tile([P, 3 * JC], U8, align_bytes=64)
-        nc.vector.tensor_copy(a_early[:], tab_a_scales[:].bitcast(U8).indirect(list_a[:, 0:24]))
-        a_words = [area.tile([P, JC], U32, name="a_words_0", align_bytes=64, offset=0)]
-        a_words.extend(keep.tile([P, JC], U32, name="a_words_%d" % c, align_bytes=64) for c in range(1, CHUNKS))
-        for c in range(CHUNKS):
-            nc.vector.tensor_copy(a_words[c][:], tab_a_words[:].bitcast(U32).indirect(list_a[:, 8 * c : 8 * (c + 1)]))
+        def quantize_wa(t0, t1):
+            cols = slice(P * t0, P * t1)
+            nc.vector.quantize_mx(
+                out=once("wa_codes", [P, R], U32)[:, cols].bitcast(FP8X4),
+                scales=once("wa_scales", [P, R], U8)[:, cols],
+                in_=made["wa_bf"][:, t0:t1, :, :].rearrange("p t m i -> p (t m i)"),
+            )
 
-        en_bf = [keep.tile([P, HALF, PACK], BF16, name="en_bf_%d" % h, align_bytes=64) for h in range(2)]
-        nc.scalar.copy(out=en_bf[0][:].rearrange("p (c u) t -> p c t u", u=4), in_=en_raw[0][:].rearrange("p t (c u) -> p c t u", u=4))
-
-        h_bf = [keep.tile([P, JC, PACK], BF16, name="h_bf_%d" % c, align_bytes=64) for c in range(CHUNKS)]
-
-        def project_a(c, scales):
+        def project_a(c):
             for t in range(PACK):
                 cols = slice(P * t, P * (t + 1))
                 nc.tensor.matmul_mx(
                     out=diff[c][:, t, :],
-                    lhsT=wa_codes[:, cols].bitcast(FP8X4),
-                    lhsT_scale=wa_scales[:, cols],
-                    rhs=a_words[c][:].bitcast(FP8X4),
-                    rhs_scale=scales,
+                    lhsT=made["wa_codes"][:, cols].bitcast(FP8X4),
+                    lhsT_scale=made["wa_scales"][:, cols],
+                    rhs=picked[("a_words", c)].bitcast(FP8X4),
+                    rhs_scale=picked[("a_scales", c)],
                     start=False,
                     stop=(t == PACK - 1),
                 )
 
-        for c in range(CHUNKS - 1):
-            project_a(c, a_early[:, JC * c : JC * (c + 1)])
-        a_late = area.tile([P, JC], U8, name="a_late", align_bytes=64, offset=0)
-        nc.vector.tensor_copy(a_late[:], tab_a_scales[:].bitcast(U8).indirect(list_a[:, 24:32]))
-        project_a(CHUNKS - 1, a_late[:])
-        for c in range(CHUNKS):
-            nc.scalar.activation(out=h_bf[c][:], in_=diff[c][:].rearrange("p t j -> p j t"), func=ACT.Abs)
+        def rectify(c):
+            nc.scalar.activation(out=once("h_bf_%d" % c, [P, JC, PACK], BF16)[:], in_=diff[c][:].rearrange("p t j -> p j t"), func=ACT.Abs)
 
-        en_codes = [keep.tile([P, HALF], U32, name="en_codes_%d" % h, align_bytes=64) for h in range(2)]
-        en_scales = [
-            area.tile([P, HALF], U8, name="en_scales_0", align_bytes=64, offset=128),
-            keep.tile([P, HALF], U8, name="en_scales_1", align_bytes=64),
-        ]
-        h_codes = keep.tile([P, J], U32, align_bytes=64)
-        h_scales = keep.tile([P, J], U8, align_bytes=64)
+        def round_en(engine, n0, n1):
+            half = n0 // HALF
+            ns = slice(n0 - HALF * half, n1 - HALF * half)
+            dst = once("en_bf_%d" % half, [P, HALF, PACK], BF16)[:, ns, :].rearrange("p (c u) t -> p c t u", u=4)
+            src = en_raw[half][:, :, ns].rearrange("p t (c u) -> p c t u", u=4)
+            if engine == "scalar":
+                nc.scalar.copy(out=dst, in_=src)
+            elif engine == "gpsimd":
+                nc.gpsimd.tensor_scalar(
+                    out=made["en_bf_%d" % half][:, ns, :],
+                    in0=en_raw[half][:, :, ns].rearrange("p t n -> p n t"),
+                    scalar1=1.0,
+                    scalar2=0.0,
+                    op0=mybir.AluOpType.mult,
+                    op1=mybir.AluOpType.add,
+                )
+            else:
+                nc.vector.tensor_copy(out=dst, in_=src)
 
         def quantize_h(c):
             js = slice(JC * c, JC * (c + 1))
-            nc.vector.quantize_mx(out=h_codes[:, js].bitcast(FP8X4), scales=h_scales[:, js], in_=h_bf[c][:].rearrange("p j t -> p (j t)"))
+            nc.vector.quantize_mx(
+                out=once("h_codes", [P, J], U32)[:, js].bitcast(FP8X4),
+                scales=once("h_scales", [P, J], U8)[:, js],
+                in_=made["h_bf_%d" % c][:].rearrange("p j t -> p (j t)"),
+            )
 
         def quantize_en(half):
-            nc.vector.quantize_mx(out=en_codes[half][:].bitcast(FP8X4), scales=en_scales[half][:], in_=en_bf[half][:].rearrange("p n t -> p (n t)"))
-
-        def score(j0, m, engine):
-            js = slice(j0, j0 + HALF)
-            ns = slice(P * (m % 2), P * (m % 2 + 1))
-            y = psum.tile([P, HALF], F32, name="bank")
-            nc.tensor.matmul_mx(
-                out=y[:],
-                lhsT=en_codes[m // 2][:, ns].bitcast(FP8X4),
-                lhsT_scale=en_scales[m // 2][:, ns],
-                rhs=h_codes[:, js].bitcast(FP8X4),
-                rhs_scale=h_scales[:, js],
-                start=True,
-                stop=True,
+            nc.vector.quantize_mx(
+                out=once("en_codes_%d" % half, [P, HALF], U32)[:].bitcast(FP8X4),
+                scales=once("en_scales_%d" % half, [P, HALF], U8)[:],
+                in_=made["en_bf_%d" % half][:].rearrange("p n t -> p (n t)"),
             )
-            staged = keep.tile([P, HALF], F32, name="staged_%d_%d" % (j0, m))
+
+        banks = {}
+
+        def score(j0, width, m0, count):
+            js = slice(j0, j0 + width)
+            y = psum.tile([P, count, width], F32, name="bank")
+            banks.update({(j0, m0): (y, width, count)})
+            for m in range(m0, m0 + count):
+                ns = slice(P * (m % 2), P * (m % 2 + 1))
+                nc.tensor.matmul_mx(
+                    out=y[:, m - m0, :],
+                    lhsT=made["en_codes_%d" % (m // 2)][:, ns].bitcast(FP8X4),
+                    lhsT_scale=made["en_scales_%d" % (m // 2)][:, ns],
+                    rhs=made["h_codes"][:, js].bitcast(FP8X4),
+                    rhs_scale=made["h_scales"][:, js],
+                    start=True,
+                    stop=True,
+                )
+
+        def leave(j0, m0, engine, queue):
+            y, width, count = banks[(j0, m0)]
+            staged = sbuf("staged_%d_%d" % (j0, m0), [P, count, width], F32)
             if engine == "vector":
                 nc.vector.tensor_copy(out=staged[:], in_=y[:])
             else:
                 nc.scalar.copy(out=staged[:], in_=y[:])
-            nc.sync.dma_start(out=out[P * m : P * (m + 1), js], in_=staged[:])
+            queue.dma_start(out=out[P * m0 : P * (m0 + count), j0 : j0 + width].rearrange("(m p) j -> p m j", p=P), in_=staged[:])
 
-        def round_en(n0, n1):
-            nc.vector.tensor_copy(
-                out=en_bf[1][:, n0:n1, :].rearrange("p (c u) t -> p c t u", u=4),
-                in_=en_raw[1][:, :, n0:n1].rearrange("p t (c u) -> p c t u", u=4),
-            )
-
+        nc.vector.memset(tab_b_scales[:], 0)
+        nc.vector.memset(wb_scales_raw[:], 0)
+        nc.vector.memset(tab_a_scales[:], 0)
+        nc.sync.dma_start(list_b[:], offs2)
+        nc.sync.dma_start(out=wb_words_raw[:], in_=wb_words[0].bitcast(I32))
+        nc.sync.dma_start(list_a[:], offs)
+        load_scale_rows(mixed4, tab_b_scales, tab2_scales)
+        load_words(tab_b_words, tab2_words)
+        load_half(wa_raw, wa_rows, 0)
+        load_scale_rows(sync4, wb_scales_raw, wb_scales)
+        load_half(wa_raw, wa_rows, 1)
+        load_half(en_raw, en_rows, 0)
+        load_scale_rows(sync4, tab_a_scales, tab_scales)
+        load_words(tab_a_words, tab_words)
+        load_half(en_raw, en_rows, 1)
+        round_wa("scalar", 0, 64)
+        round_wa("scalar", 64, 84)
+        deal_wb_words()
+        gather("b_scales", 0, 4)
+        gather("b_words", 0, 4)
+        deal_wb_scales()
+        project_b(0)
+        project_b(1)
+        project_b(2)
+        project_b(3)
+        round_wa("vector", 84, 128)
+        quantize_wa(0, 4)
+        gather("a_scales", 0, 3)
+        round_en("scalar", 0, 256)
+        gather("a_words", 0, 1)
+        gather("a_words", 1, 2)
+        gather("a_words", 2, 3)
+        gather("a_words", 3, 4)
+        project_a(0)
+        project_a(1)
+        project_a(2)
+        gather("a_scales", 3, 4)
+        project_a(3)
+        rectify(0)
+        rectify(1)
+        rectify(2)
+        rectify(3)
         quantize_en(0)
         quantize_h(0)
         quantize_h(1)
-        round_en(0, P)
-        round_en(P, HALF)
-        score(0, 0, "vector")
+        round_en("vector", 256, 384)
+        round_en("vector", 384, 512)
+        score(0, 256, 0, 1)
+        score(0, 256, 1, 1)
         quantize_en(1)
+        score(0, 256, 2, 1)
+        score(0, 256, 3, 1)
         quantize_h(2)
         quantize_h(3)
-        score(0, 1, "scalar")
-        score(0, 2, "scalar")
-        score(0, 3, "scalar")
-        score(HALF, 0, "vector")
-        score(HALF, 1, "vector")
-        score(HALF, 2, "scalar")
-        score(HALF, 3, "vector")
+        score(256, 256, 0, 1)
+        score(256, 256, 1, 1)
+        score(256, 256, 2, 1)
+        score(256, 256, 3, 1)
+        leave(0, 0, "scalar", nc.sync)
+        leave(0, 1, "scalar", nc.sync)
+        leave(0, 2, "vector", nc.sync)
+        leave(0, 3, "scalar", nc.sync)
+        leave(256, 0, "vector", nc.sync)
+        leave(256, 1, "scalar", nc.sync)
+        leave(256, 2, "vector", nc.sync)
+        leave(256, 3, "scalar", nc.sync)

@@ -21,6 +21,7 @@ JC = 128
 CHUNKS = J // JC
 HALF = 256
 WA_SCALAR_END = 84
+EN_CUTS = (0, 256, 384, 512)
 
 
 def tile_list_kg_absd_none_kernel(tc, tab_words, tab_scales, tab2_words, tab2_scales, wa, wb_words, wb_scales, en, offs, offs2, out):
@@ -29,7 +30,7 @@ def tile_list_kg_absd_none_kernel(tc, tab_words, tab_scales, tab2_words, tab2_sc
         keep = ctx.enter_context(tc.tile_pool(name="keep", bufs=1))
         area = ctx.enter_context(tc.tile_pool(name="area", bufs=1))
         psum = ctx.enter_context(tc.psum_pool(name="psum", bufs=8))
-        placed = {"a_words_0": 0, "a_scales_3": 0, "en_scales_0": 128, "h_bf_3": 1024, "staged_0_2": 1024}
+        placed = {"a_words_0": 0, "a_scales_3": 0, "en_scales_0": 128, "h_first": 1024, "en_raw_1": 1536, "h_rest": 2048, "en_codes_1": 1024, "staged_128_2": 3072, "staged_256_0": 4096}
 
         def sbuf(name, shape, dtype):
             if name in placed:
@@ -52,10 +53,9 @@ def tile_list_kg_absd_none_kernel(tc, tab_words, tab_scales, tab2_words, tab2_sc
         wa_rows = wa.rearrange("(p i) r -> p i r", i=PACK)
         en_rows = en.rearrange("(p t) n -> p t n", t=PACK)
         wa_raw = [sbuf("wa_raw_%d" % h, [P, PACK, HALF], F32) for h in range(2)]
-        en_raw = [sbuf("en_raw_%d" % h, [P, PACK, HALF], F32) for h in range(2)]
+        en_raw = [sbuf("en_raw_%d" % h, [P, PACK, EN_CUTS[h + 1] - EN_CUTS[h]], F32) for h in range(3)]
         sync4 = (nc.sync, nc.sync, nc.sync, nc.sync)
         mixed4 = (nc.sync, nc.sync, nc.scalar, nc.scalar)
-        scalar4 = (nc.scalar, nc.scalar, nc.scalar, nc.scalar)
         made = {}
 
         def once(name, shape, dtype):
@@ -68,6 +68,9 @@ def tile_list_kg_absd_none_kernel(tc, tab_words, tab_scales, tab2_words, tab2_sc
 
         def load_half(tiles, rows, h):
             nc.sync.dma_start(out=tiles[h][:], in_=rows[:, :, HALF * h : HALF * (h + 1)])
+
+        def load_en(h):
+            nc.sync.dma_start(out=en_raw[h][:], in_=en_rows[:, :, EN_CUTS[h] : EN_CUTS[h + 1]])
 
         def round_wa(engine, m0, m1):
             half = m0 // 64
@@ -139,25 +142,21 @@ def tile_list_kg_absd_none_kernel(tc, tab_words, tab_scales, tab2_words, tab2_sc
                     stop=(t == PACK - 1),
                 )
 
-        def rectify(c):
-            nc.scalar.activation(out=once("h_bf_%d" % c, [P, JC, PACK], BF16)[:], in_=diff[c][:].rearrange("p t j -> p j t"), func=ACT.Abs)
+        def h_chunk(c):
+            if c == 0:
+                return once("h_first", [P, JC, PACK], BF16)[:]
+            return once("h_rest", [P, J - JC, PACK], BF16)[:, JC * (c - 1) : JC * c, :]
 
-        def round_en(engine, n0, n1):
-            half = n0 // HALF
-            ns = slice(n0 - HALF * half, n1 - HALF * half)
+        def rectify(c):
+            nc.scalar.activation(out=h_chunk(c), in_=diff[c][:].rearrange("p t j -> p j t"), func=ACT.Abs)
+
+        def round_en(engine, h):
+            half = EN_CUTS[h] // HALF
+            ns = slice(EN_CUTS[h] - HALF * half, EN_CUTS[h + 1] - HALF * half)
             dst = once("en_bf_%d" % half, [P, HALF, PACK], BF16)[:, ns, :].rearrange("p (c u) t -> p c t u", u=4)
-            src = en_raw[half][:, :, ns].rearrange("p t (c u) -> p c t u", u=4)
+            src = en_raw[h][:].rearrange("p t (c u) -> p c t u", u=4)
             if engine == "scalar":
                 nc.scalar.copy(out=dst, in_=src)
-            elif engine == "gpsimd":
-                nc.gpsimd.tensor_scalar(
-                    out=made["en_bf_%d" % half][:, ns, :],
-                    in0=en_raw[half][:, :, ns].rearrange("p t n -> p n t"),
-                    scalar1=1.0,
-                    scalar2=0.0,
-                    op0=mybir.AluOpType.mult,
-                    op1=mybir.AluOpType.add,
-                )
             else:
                 nc.vector.tensor_copy(out=dst, in_=src)
 
@@ -166,7 +165,7 @@ def tile_list_kg_absd_none_kernel(tc, tab_words, tab_scales, tab2_words, tab2_sc
             nc.vector.quantize_mx(
                 out=once("h_codes", [P, J], U32)[:, js].bitcast(FP8X4),
                 scales=once("h_scales", [P, J], U8)[:, js],
-                in_=made["h_bf_%d" % c][:].rearrange("p j t -> p (j t)"),
+                in_=h_chunk(c).rearrange("p j t -> p (j t)"),
             )
 
         def quantize_en(half):
@@ -214,10 +213,11 @@ def tile_list_kg_absd_none_kernel(tc, tab_words, tab_scales, tab2_words, tab2_sc
         load_half(wa_raw, wa_rows, 0)
         load_scale_rows(sync4, wb_scales_raw, wb_scales)
         load_half(wa_raw, wa_rows, 1)
-        load_half(en_raw, en_rows, 0)
+        load_en(0)
         load_scale_rows(sync4, tab_a_scales, tab_scales)
         load_words(tab_a_words, tab_words)
-        load_half(en_raw, en_rows, 1)
+        load_en(1)
+        load_en(2)
         round_wa("scalar", 0, 64)
         round_wa("scalar", 64, 84)
         deal_wb_words()
@@ -231,7 +231,8 @@ def tile_list_kg_absd_none_kernel(tc, tab_words, tab_scales, tab2_words, tab2_sc
         round_wa("vector", 84, 128)
         quantize_wa(0, 4)
         gather("a_scales", 0, 3)
-        round_en("scalar", 0, 256)
+        round_en("scalar", 0)
+        round_en("scalar", 1)
         gather("a_words", 0, 1)
         gather("a_words", 1, 2)
         gather("a_words", 2, 3)
@@ -245,27 +246,27 @@ def tile_list_kg_absd_none_kernel(tc, tab_words, tab_scales, tab2_words, tab2_sc
         rectify(1)
         rectify(2)
         rectify(3)
+
         quantize_en(0)
+        round_en("vector", 2)
         quantize_h(0)
+        score(0, 128, 0, 2)
         quantize_h(1)
-        round_en("vector", 256, 384)
-        round_en("vector", 384, 512)
-        score(0, 256, 0, 1)
-        score(0, 256, 1, 1)
+        score(128, 128, 0, 2)
         quantize_en(1)
-        score(0, 256, 2, 1)
-        score(0, 256, 3, 1)
+        score(0, 128, 2, 2)
+        score(128, 128, 2, 2)
+        leave(0, 0, "vector", nc.sync)
         quantize_h(2)
+        score(256, 128, 0, 2)
+        score(256, 128, 2, 2)
         quantize_h(3)
-        score(256, 256, 0, 1)
-        score(256, 256, 1, 1)
-        score(256, 256, 2, 1)
-        score(256, 256, 3, 1)
-        leave(0, 0, "scalar", nc.sync)
-        leave(0, 1, "scalar", nc.sync)
-        leave(0, 2, "vector", nc.sync)
-        leave(0, 3, "scalar", nc.sync)
+        score(384, 128, 0, 2)
+        score(384, 128, 2, 2)
+        leave(128, 0, "scalar", nc.sync)
+        leave(0, 2, "scalar", nc.sync)
+        leave(128, 2, "vector", nc.sync)
         leave(256, 0, "vector", nc.sync)
-        leave(256, 1, "scalar", nc.sync)
-        leave(256, 2, "vector", nc.sync)
-        leave(256, 3, "scalar", nc.sync)
+        leave(256, 2, "scalar", nc.sync)
+        leave(384, 0, "vector", nc.sync)
+        leave(384, 2, "scalar", nc.sync)

@@ -30,7 +30,7 @@ def tile_list_kg_absd_none_kernel(tc, tab_words, tab_scales, tab2_words, tab2_sc
         keep = ctx.enter_context(tc.tile_pool(name="keep", bufs=1))
         area = ctx.enter_context(tc.tile_pool(name="area", bufs=1))
         psum = ctx.enter_context(tc.psum_pool(name="psum", bufs=8))
-        placed = {"a_words_0": 0, "a_scales_3": 0, "en_scales_0": 128, "h_first": 1024, "en_raw_1": 1536, "h_rest": 2048, "en_codes_1": 1024, "staged_128_2": 3072, "staged_256_0": 4096}
+        placed = {"a_words_0": 0, "a_scales_3": 0, "en_scales_0": 128, "h_first": 1024, "en_raw_1": 1536, "h_rest": 2048, "en_codes_1": 1024, "staged_0_3": 3072}
 
         def sbuf(name, shape, dtype):
             if name in placed:
@@ -251,22 +251,22 @@ def tile_list_kg_absd_none_kernel(tc, tab_words, tab_scales, tab2_words, tab2_sc
         round_en("vector", 2)
         quantize_h(0)
         score(0, 128, 0, 2)
+        quantize_en(1)
         quantize_h(1)
         score(128, 128, 0, 2)
-        quantize_en(1)
-        score(0, 128, 2, 2)
-        score(128, 128, 2, 2)
+        score(0, 256, 2, 1)
+        score(0, 256, 3, 1)
         leave(0, 0, "vector", nc.sync)
         quantize_h(2)
-        score(256, 128, 0, 2)
-        score(256, 128, 2, 2)
         quantize_h(3)
-        score(384, 128, 0, 2)
-        score(384, 128, 2, 2)
+        score(256, 256, 0, 1)
+        score(256, 256, 1, 1)
+        score(256, 256, 2, 1)
+        score(256, 256, 3, 1)
         leave(128, 0, "scalar", nc.sync)
         leave(0, 2, "scalar", nc.sync)
-        leave(128, 2, "vector", nc.sync)
+        leave(0, 3, "vector", nc.sync)
         leave(256, 0, "vector", nc.sync)
-        leave(256, 2, "scalar", nc.sync)
-        leave(384, 0, "vector", nc.sync)
-        leave(384, 2, "scalar", nc.sync)
+        leave(256, 1, "scalar", nc.sync)
+        leave(256, 2, "vector", nc.sync)
+        leave(256, 3, "scalar", nc.sync)

@@ -20,7 +20,6 @@ PACK = 4
 JC = 128
 CHUNKS = J // JC
 HALF = 256
-WA_SCALAR_END = 84
 EN_CUTS = (0, 256, 384, 512)
 
 
@@ -52,7 +51,7 @@ def tile_list_kg_absd_none_kernel(tc, tab_words, tab_scales, tab2_words, tab2_sc
         wb_words_raw = sbuf("wb_words_raw", [P, R // 2], I32)
         wa_rows = wa.rearrange("(p i) r -> p i r", i=PACK)
         en_rows = en.rearrange("(p t) n -> p t n", t=PACK)
-        wa_raw = [sbuf("wa_raw_%d" % h, [P, PACK, HALF], F32) for h in range(2)]
+        wa_raw = [sbuf("wa_raw_%d" % h, [P, 2, R], F32) for h in range(2)]
         en_raw = [sbuf("en_raw_%d" % h, [P, PACK, EN_CUTS[h + 1] - EN_CUTS[h]], F32) for h in range(3)]
         sync4 = (nc.sync, nc.sync, nc.sync, nc.sync)
         mixed4 = (nc.sync, nc.sync, nc.scalar, nc.scalar)
@@ -67,15 +66,14 @@ def tile_list_kg_absd_none_kernel(tc, tab_words, tab_scales, tab2_words, tab2_sc
             nc.sync.dma_start(out=tile[:], in_=words[0].rearrange("p t i -> p (t i)").bitcast(I32))
 
         def load_half(tiles, rows, h):
-            nc.sync.dma_start(out=tiles[h][:], in_=rows[:, :, HALF * h : HALF * (h + 1)])
+            nc.sync.dma_start(out=tiles[h][:], in_=rows[:, 2 * h : 2 * h + 2, :])
 
         def load_en(h):
             nc.sync.dma_start(out=en_raw[h][:], in_=en_rows[:, :, EN_CUTS[h] : EN_CUTS[h + 1]])
 
-        def round_wa(engine, m0, m1):
-            half = m0 // 64
-            src = wa_raw[half][:, :, PACK * m0 - HALF * half : PACK * m1 - HALF * half].rearrange("p i (m t) -> p m t i", t=PACK)
-            dst = once("wa_bf", [P, PACK, P, PACK], BF16)[:, :, m0:m1, :].rearrange("p t m i -> p m t i")
+        def round_wa(engine, pair):
+            src = wa_raw[pair][:].rearrange("p i (m t) -> p m t i", t=PACK)
+            dst = once("wa_bf", [P, PACK, P, PACK], BF16)[:, :, :, 2 * pair : 2 * pair + 2].rearrange("p t m i -> p m t i")
             if engine == "scalar":
                 nc.scalar.activation(out=dst, in_=src, func=ACT.Copy, scale=-1.0)
             else:
@@ -218,8 +216,7 @@ def tile_list_kg_absd_none_kernel(tc, tab_words, tab_scales, tab2_words, tab2_sc
         load_words(tab_a_words, tab_words)
         load_en(1)
         load_en(2)
-        round_wa("scalar", 0, 64)
-        round_wa("scalar", 64, 84)
+        round_wa("scalar", 0)
         deal_wb_words()
         gather("b_scales", 0, 4)
         gather("b_words", 0, 4)
@@ -228,7 +225,7 @@ def tile_list_kg_absd_none_kernel(tc, tab_words, tab_scales, tab2_words, tab2_sc
         project_b(1)
         project_b(2)
         project_b(3)
-        round_wa("vector", 84, 128)
+        round_wa("vector", 1)
         quantize_wa(0, 4)
         gather("a_scales", 0, 3)
         round_en("scalar", 0)

@@ -20,6 +20,7 @@ PACK = 4
 JC = 128
 CHUNKS = J // JC
 HALF = 256
+WA_ON_SCALAR = 56
 EN_CUTS = (0, 256, 384, 512)
 
 
@@ -51,7 +52,7 @@ def tile_list_kg_absd_none_kernel(tc, tab_words, tab_scales, tab2_words, tab2_sc
         wb_words_raw = sbuf("wb_words_raw", [P, R // 2], I32)
         wa_rows = wa.rearrange("(p i) r -> p i r", i=PACK)
         en_rows = en.rearrange("(p t) n -> p t n", t=PACK)
-        wa_raw = [sbuf("wa_raw_%d" % h, [P, 2, R], F32) for h in range(2)]
+        wa_raw = sbuf("wa_raw", [P, PACK, R], F32)
         en_raw = [sbuf("en_raw_%d" % h, [P, PACK, EN_CUTS[h + 1] - EN_CUTS[h]], F32) for h in range(3)]
         sync4 = (nc.sync, nc.sync, nc.sync, nc.sync)
         mixed4 = (nc.sync, nc.sync, nc.scalar, nc.scalar)
@@ -65,15 +66,15 @@ def tile_list_kg_absd_none_kernel(tc, tab_words, tab_scales, tab2_words, tab2_sc
         def load_words(tile, words):
             nc.sync.dma_start(out=tile[:], in_=words[0].rearrange("p t i -> p (t i)").bitcast(I32))
 
-        def load_half(tiles, rows, h):
-            nc.sync.dma_start(out=tiles[h][:], in_=rows[:, 2 * h : 2 * h + 2, :])
+        def load_wa(pair):
+            nc.sync.dma_start(out=wa_raw[:, 2 * pair : 2 * pair + 2, :], in_=wa_rows[:, 2 * pair : 2 * pair + 2, :])
 
         def load_en(h):
             nc.sync.dma_start(out=en_raw[h][:], in_=en_rows[:, :, EN_CUTS[h] : EN_CUTS[h + 1]])
 
-        def round_wa(engine, pair):
-            src = wa_raw[pair][:].rearrange("p i (m t) -> p m t i", t=PACK)
-            dst = once("wa_bf", [P, PACK, P, PACK], BF16)[:, :, :, 2 * pair : 2 * pair + 2].rearrange("p t m i -> p m t i")
+        def round_wa(engine, i0, i1, m0, m1):
+            src = wa_raw[:, i0:i1, PACK * m0 : PACK * m1].rearrange("p i (m t) -> p m t i", t=PACK)
+            dst = once("wa_bf", [P, PACK, P, PACK], BF16)[:, :, m0:m1, i0:i1].rearrange("p t m i -> p m t i")
             if engine == "scalar":
                 nc.scalar.activation(out=dst, in_=src, func=ACT.Copy, scale=-1.0)
             else:
@@ -208,15 +209,16 @@ def tile_list_kg_absd_none_kernel(tc, tab_words, tab_scales, tab2_words, tab2_sc
         nc.sync.dma_start(list_a[:], offs)
         load_scale_rows(mixed4, tab_b_scales, tab2_scales)
         load_words(tab_b_words, tab2_words)
-        load_half(wa_raw, wa_rows, 0)
+        load_wa(0)
         load_scale_rows(sync4, wb_scales_raw, wb_scales)
-        load_half(wa_raw, wa_rows, 1)
+        load_wa(1)
         load_en(0)
         load_scale_rows(sync4, tab_a_scales, tab_scales)
         load_words(tab_a_words, tab_words)
         load_en(1)
         load_en(2)
-        round_wa("scalar", 0)
+        round_wa("scalar", 0, 2, 0, WA_ON_SCALAR)
+        round_wa("scalar", 2, 4, 0, WA_ON_SCALAR)
         deal_wb_words()
         gather("b_scales", 0, 4)
         gather("b_words", 0, 4)
@@ -225,7 +227,7 @@ def tile_list_kg_absd_none_kernel(tc, tab_words, tab_scales, tab2_words, tab2_sc
         project_b(1)
         project_b(2)
         project_b(3)
-        round_wa("vector", 1)
+        round_wa("vector", 0, 4, WA_ON_SCALAR, P)
         quantize_wa(0, 4)
         gather("a_scales", 0, 3)
         round_en("scalar", 0)

@@ -88,8 +88,8 @@ def tile_list_kg_absd_none_kernel(tc, tab_words, tab_scales, tab2_words, tab2_sc
 
         def deal_wb_scales():
             nc.vector.tensor_copy(
-                out=once("wb_plane", [P, R], U8)[:].rearrange("p (t m) -> p m t", t=PACK),
-                in_=wb_scales_raw[:].bitcast(U8).rearrange("p (m t) -> p m t", t=PACK),
+                out=once("wb_plane", [P, R], U8)[:].rearrange("p (t m) -> p t m", t=PACK),
+                in_=wb_scales_raw[:].bitcast(U8).rearrange("p (m t) -> p t m", t=PACK),
             )
 
         picked = {}
@@ -176,14 +176,16 @@ def tile_list_kg_absd_none_kernel(tc, tab_words, tab_scales, tab2_words, tab2_sc
 
         banks = {}
 
-        def score(j0, width, m0, count):
-            js = slice(j0, j0 + width)
-            y = psum.tile([P, count, width], F32, name="bank")
-            banks.update({(j0, m0): (y, width, count)})
+        def score(j0, width, m0, count, part=None):
+            if (j0, m0) not in banks:
+                banks.update({(j0, m0): (psum.tile([P, count, width], F32, name="bank"), width, count)})
+            y = banks[(j0, m0)][0]
+            a, b = (0, width) if part is None else (JC * part, JC * (part + 1))
+            js = slice(j0 + a, j0 + b)
             for m in range(m0, m0 + count):
                 ns = slice(P * (m % 2), P * (m % 2 + 1))
                 nc.tensor.matmul_mx(
-                    out=y[:, m - m0, :],
+                    out=y[:, m - m0, a:b],
                     lhsT=made["en_codes_%d" % (m // 2)][:, ns].bitcast(FP8X4),
                     lhsT_scale=made["en_scales_%d" % (m // 2)][:, ns],
                     rhs=made["h_codes"][:, js].bitcast(FP8X4),
@@ -257,11 +259,11 @@ def tile_list_kg_absd_none_kernel(tc, tab_words, tab_scales, tab2_words, tab2_sc
         score(0, 256, 3, 1)
         leave(0, 0, "vector", nc.sync)
         quantize_h(2)
+        for m in range(4):
+            score(256, 256, m, 1, 0)
         quantize_h(3)
-        score(256, 256, 0, 1)
-        score(256, 256, 1, 1)
-        score(256, 256, 2, 1)
-        score(256, 256, 3, 1)
+        for m in range(4):
+            score(256, 256, m, 1, 1)
         leave(128, 0, "scalar", nc.sync)
         leave(0, 2, "scalar", nc.sync)
         leave(0, 3, "vector", nc.sync)

@@ -154,7 +154,9 @@ def tile_list_kg_absd_none_kernel(tc, tab_words, tab_scales, tab2_words, tab2_sc
             ns = slice(EN_CUTS[h] - HALF * half, EN_CUTS[h + 1] - HALF * half)
             dst = once("en_bf_%d" % half, [P, HALF, PACK], BF16)[:, ns, :].rearrange("p (c u) t -> p c t u", u=4)
             src = en_raw[h][:].rearrange("p t (c u) -> p c t u", u=4)
-            if engine == "scalar":
+            if engine == "gpsimd":
+                nc.gpsimd.tensor_scalar(made["en_bf_%d" % half][:, ns, :], en_raw[h][:].rearrange("p t n -> p n t"), 1.0, 0.0, mybir.AluOpType.mult, mybir.AluOpType.add)
+            elif engine == "scalar":
                 nc.scalar.copy(out=dst, in_=src)
             else:
                 nc.vector.tensor_copy(out=dst, in_=src)
@@ -206,15 +208,15 @@ def tile_list_kg_absd_none_kernel(tc, tab_words, tab_scales, tab2_words, tab2_sc
         nc.vector.memset(tab_b_scales[:], 0)
         nc.vector.memset(wb_scales_raw[:], 0)
         nc.vector.memset(tab_a_scales[:], 0)
-        nc.sync.dma_start(list_b[:], offs2)
         nc.sync.dma_start(out=wb_words_raw[:], in_=wb_words[0].bitcast(I32))
-        nc.sync.dma_start(list_a[:], offs)
+        nc.sync.dma_start(list_b[:], offs2)
         load_scale_rows(mixed4, tab_b_scales, tab2_scales)
         load_words(tab_b_words, tab2_words)
         load_wa(0)
         load_scale_rows(sync4, wb_scales_raw, wb_scales)
         load_wa(1)
         load_en(0)
+        nc.sync.dma_start(list_a[:], offs)
         load_scale_rows(sync4, tab_a_scales, tab_scales)
         load_words(tab_a_words, tab_words)
         load_en(1)
@@ -249,7 +251,7 @@ def tile_list_kg_absd_none_kernel(tc, tab_words, tab_scales, tab2_words, tab2_sc
         rectify(3)
 
         quantize_en(0)
-        round_en("vector", 2)
+        round_en("gpsimd", 2)
         quantize_h(0)
         score(0, 128, 0, 2)
         quantize_en(1)

@@ -21,7 +21,8 @@ JC = 128
 CHUNKS = J // JC
 HALF = 256
 WA_ON_SCALAR = 56
-EN_CUTS = (0, 256, 384, 512)
+EN_ON_GPSIMD = 160
+EN_CUTS = (0, 256, 512)
 
 
 def tile_list_kg_absd_none_kernel(tc, tab_words, tab_scales, tab2_words, tab2_scales, wa, wb_words, wb_scales, en, offs, offs2, out):
@@ -30,7 +31,7 @@ def tile_list_kg_absd_none_kernel(tc, tab_words, tab_scales, tab2_words, tab2_sc
         keep = ctx.enter_context(tc.tile_pool(name="keep", bufs=1))
         area = ctx.enter_context(tc.tile_pool(name="area", bufs=1))
         psum = ctx.enter_context(tc.psum_pool(name="psum", bufs=8))
-        placed = {"a_words_0": 0, "a_scales_3": 0, "en_scales_0": 128, "h_first": 1024, "en_raw_1": 1536, "h_rest": 2048, "en_codes_1": 1024, "staged_0_3": 3072}
+        placed = {"a_words_0": 0, "a_scales_2": 0, "a_scales_3": 128, "en_scales_0": 256, "en_raw_0": 1024, "h_first": 1024, "h_rest": 2048, "en_codes_1": 1024, "staged_0_3": 3072}
 
         def sbuf(name, shape, dtype):
             if name in placed:
@@ -53,7 +54,7 @@ def tile_list_kg_absd_none_kernel(tc, tab_words, tab_scales, tab2_words, tab2_sc
         wa_rows = wa.rearrange("(p i) r -> p i r", i=PACK)
         en_rows = en.rearrange("(p t) n -> p t n", t=PACK)
         wa_raw = sbuf("wa_raw", [P, PACK, R], F32)
-        en_raw = [sbuf("en_raw_%d" % h, [P, PACK, EN_CUTS[h + 1] - EN_CUTS[h]], F32) for h in range(3)]
+        en_raw = [sbuf("en_raw_%d" % h, [P, PACK, EN_CUTS[h + 1] - EN_CUTS[h]], F32) for h in range(2)]
         sync4 = (nc.sync, nc.sync, nc.sync, nc.sync)
         mixed4 = (nc.sync, nc.sync, nc.scalar, nc.scalar)
         made = {}
@@ -149,17 +150,15 @@ def tile_list_kg_absd_none_kernel(tc, tab_words, tab_scales, tab2_words, tab2_sc
         def rectify(c):
             nc.scalar.activation(out=h_chunk(c), in_=diff[c][:].rearrange("p t j -> p j t"), func=ACT.Abs)
 
-        def round_en(engine, h):
-            half = EN_CUTS[h] // HALF
-            ns = slice(EN_CUTS[h] - HALF * half, EN_CUTS[h + 1] - HALF * half)
-            dst = once("en_bf_%d" % half, [P, HALF, PACK], BF16)[:, ns, :].rearrange("p (c u) t -> p c t u", u=4)
-            src = en_raw[h][:].rearrange("p t (c u) -> p c t u", u=4)
+        def round_en(engine, half, n0, n1):
+            dst = once("en_bf_%d" % half, [P, HALF, PACK], BF16)[:, n0:n1, :]
+            src = en_raw[half][:, :, n0:n1]
             if engine == "gpsimd":
-                nc.gpsimd.tensor_scalar(made["en_bf_%d" % half][:, ns, :], en_raw[h][:].rearrange("p t n -> p n t"), 1.0, 0.0, mybir.AluOpType.mult, mybir.AluOpType.add)
+                nc.gpsimd.tensor_scalar(dst, src.rearrange("p t n -> p n t"), 1.0, 0.0, mybir.AluOpType.mult, mybir.AluOpType.add)
             elif engine == "scalar":
-                nc.scalar.copy(out=dst, in_=src)
+                nc.scalar.copy(out=dst.rearrange("p (c u) t -> p c t u", u=4), in_=src.rearrange("p t (c u) -> p c t u", u=4))
             else:
-                nc.vector.tensor_copy(out=dst, in_=src)
+                nc.vector.tensor_copy(out=dst.rearrange("p (c u) t -> p c t u", u=4), in_=src.rearrange("p t (c u) -> p c t u", u=4))
 
         def quantize_h(c):
             js = slice(JC * c, JC * (c + 1))
@@ -220,7 +219,6 @@ def tile_list_kg_absd_none_kernel(tc, tab_words, tab_scales, tab2_words, tab2_sc
         load_scale_rows(sync4, tab_a_scales, tab_scales)
         load_words(tab_a_words, tab_words)
         load_en(1)
-        load_en(2)
         round_wa("scalar", 0, 2, 0, WA_ON_SCALAR)
         round_wa("scalar", 2, 4, 0, WA_ON_SCALAR)
         deal_wb_words()
@@ -233,15 +231,16 @@ def tile_list_kg_absd_none_kernel(tc, tab_words, tab_scales, tab2_words, tab2_sc
         project_b(3)
         round_wa("vector", 0, 4, WA_ON_SCALAR, P)
         quantize_wa(0, 4)
-        gather("a_scales", 0, 3)
-        round_en("scalar", 0)
-        round_en("scalar", 1)
+        gather("a_scales", 0, 2)
+        round_en("scalar", 0, 0, HALF)
+        round_en("gpsimd", 1, 0, EN_ON_GPSIMD)
         gather("a_words", 0, 1)
         gather("a_words", 1, 2)
         gather("a_words", 2, 3)
         gather("a_words", 3, 4)
         project_a(0)
         project_a(1)
+        gather("a_scales", 2, 3)
         project_a(2)
         gather("a_scales", 3, 4)
         project_a(3)
@@ -251,7 +250,7 @@ def tile_list_kg_absd_none_kernel(tc, tab_words, tab_scales, tab2_words, tab2_sc
         rectify(3)
 
         quantize_en(0)
-        round_en("gpsimd", 2)
+        round_en("vector", 1, EN_ON_GPSIMD, HALF)
         quantize_h(0)
         score(0, 128, 0, 2)
         quantize_en(1)

@@ -265,10 +265,10 @@ def tile_list_kg_absd_none_kernel(tc, tab_words, tab_scales, tab2_words, tab2_sc
         quantize_h(3)
         for m in range(4):
             score(256, 256, m, 1, 1)
-        leave(128, 0, "scalar", nc.sync)
-        leave(0, 2, "scalar", nc.sync)
+        leave(128, 0, "scalar", nc.scalar)
+        leave(0, 2, "scalar", nc.scalar)
         leave(0, 3, "vector", nc.sync)
         leave(256, 0, "vector", nc.sync)
-        leave(256, 1, "scalar", nc.sync)
+        leave(256, 1, "scalar", nc.scalar)
         leave(256, 2, "vector", nc.sync)
-        leave(256, 3, "scalar", nc.sync)
+        leave(256, 3, "scalar", nc.scalar)

@@ -252,10 +252,10 @@ def tile_list_kg_absd_none_kernel(tc, tab_words, tab_scales, tab2_words, tab2_sc
         quantize_en(0)
         round_en("vector", 1, EN_ON_GPSIMD, HALF)
         quantize_h(0)
-        score(0, 128, 0, 2)
         quantize_en(1)
         quantize_h(1)
-        score(128, 128, 0, 2)
+        score(0, 256, 0, 1)
+        score(0, 256, 1, 1)
         score(0, 256, 2, 1)
         score(0, 256, 3, 1)
         leave(0, 0, "vector", nc.sync)
@@ -265,7 +265,7 @@ def tile_list_kg_absd_none_kernel(tc, tab_words, tab_scales, tab2_words, tab2_sc
         quantize_h(3)
         for m in range(4):
             score(256, 256, m, 1, 1)
-        leave(128, 0, "scalar", nc.scalar)
+        leave(0, 1, "scalar", nc.scalar)
         leave(0, 2, "scalar", nc.scalar)
         leave(0, 3, "vector", nc.sync)
         leave(256, 0, "vector", nc.sync)

@@ -23,6 +23,7 @@ HALF = 256
 WA_ON_SCALAR = 56
 EN_ON_GPSIMD = 160
 EN_CUTS = (0, 256, 512)
+A_PLANE = 8
 
 
 def tile_list_kg_absd_none_kernel(tc, tab_words, tab_scales, tab2_words, tab2_scales, wa, wb_words, wb_scales, en, offs, offs2, out):
@@ -38,10 +39,10 @@ def tile_list_kg_absd_none_kernel(tc, tab_words, tab_scales, tab2_words, tab2_sc
                 return area.tile(shape, dtype, name=name, align_bytes=64, offset=placed[name])
             return keep.tile(shape, dtype, name=name, align_bytes=64)
 
-        def load_scale_rows(engines, tile, scales):
+        def load_scale_rows(engines, tile, scales, first=0):
             rows = scales[0].bitcast(I32)
             for quad in range(4):
-                engines[quad].dma_start(out=tile[32 * quad : 32 * quad + 4, :], in_=rows[4 * quad : 4 * quad + 4, :])
+                engines[quad].dma_start(out=tile[32 * quad + first : 32 * quad + first + 4, :], in_=rows[4 * quad : 4 * quad + 4, :])
 
         list_a = keep.tile([P, J // 16], U16, name="list_a")
         list_b = keep.tile([P, J // 16], U16, name="list_b")
@@ -105,7 +106,7 @@ def tile_list_kg_absd_none_kernel(tc, tab_words, tab_scales, tab2_words, tab2_sc
             tile = sbuf("%s_%d" % (kind, c0), [P, JC * (c1 - c0)], dtype)
             nc.vector.tensor_copy(tile[:], window[:].bitcast(dtype).indirect(offsets[:, 8 * c0 : 8 * c1]))
             for c in range(c0, c1):
-                picked.update({(kind, c): tile[:, JC * (c - c0) : JC * (c - c0 + 1)]})
+                picked.update({(kind, c): tile[(A_PLANE if kind == "a_scales" else 0) :, JC * (c - c0) : JC * (c - c0 + 1)]})
 
         diff = [psum.tile([P, PACK, JC], F32, name="bank") for c in range(CHUNKS)]
 
@@ -216,7 +217,7 @@ def tile_list_kg_absd_none_kernel(tc, tab_words, tab_scales, tab2_words, tab2_sc
         load_wa(1)
         load_en(0)
         nc.sync.dma_start(list_a[:], offs)
-        load_scale_rows(sync4, tab_a_scales, tab_scales)
+        load_scale_rows(sync4, tab_a_scales, tab_scales, A_PLANE)
         load_words(tab_a_words, tab_words)
         load_en(1)
         round_wa("scalar", 0, 2, 0, WA_ON_SCALAR)

from contextlib import ExitStack

import concourse.mybir as mybir

K, L, R, N, T, J = 512, 512, 512, 512, 1024, 512
FLOPS = 2 * (K * R * J + L * R * J + R * N * J)

F32 = mybir.dt.float32
BF16 = mybir.dt.bfloat16
I32 = mybir.dt.int32
U32 = mybir.dt.uint32
U16 = mybir.dt.uint16
U8 = mybir.dt.uint8
FP8X4 = mybir.dt.float8_e4m3fn_x4
FP4X4 = mybir.dt.float4_e2m1fn_x4
ACT = mybir.ActivationFunctionType

P = 128
PACK = 4
JC = 128
CHUNKS = J // JC
HALF = 256
WA_ON_SCALAR = 56
EN_ON_GPSIMD = 160
EN_CUTS = (0, 256, 512)
A_PLANE = 8


def tile_list_kg_absd_none_kernel(tc, tab_words, tab_scales, tab2_words, tab2_scales, wa, wb_words, wb_scales, en, offs, offs2, out):
    nc = tc.nc
    with ExitStack() as ctx:
        keep = ctx.enter_context(tc.tile_pool(name="keep", bufs=1))
        area = ctx.enter_context(tc.tile_pool(name="area", bufs=1))
        psum = ctx.enter_context(tc.psum_pool(name="psum", bufs=8))
        placed = {"a_words_0": 0, "a_scales_2": 0, "a_scales_3": 128, "en_scales_0": 256, "en_raw_0": 1024, "h_first": 1024, "h_rest": 2048, "en_codes_1": 1024, "staged_0_3": 3072}

        def sbuf(name, shape, dtype):
            if name in placed:
                return area.tile(shape, dtype, name=name, align_bytes=64, offset=placed[name])
            return keep.tile(shape, dtype, name=name, align_bytes=64)

        def load_scale_rows(engines, tile, scales, first=0):
            rows = scales[0].bitcast(I32)
            for quad in range(4):
                engines[quad].dma_start(out=tile[32 * quad + first : 32 * quad + first + 4, :], in_=rows[4 * quad : 4 * quad + 4, :])

        list_a = keep.tile([P, J // 16], U16, name="list_a")
        list_b = keep.tile([P, J // 16], U16, name="list_b")
        tab_a_scales = sbuf("tab_a_scales", [P, T // 4], I32)
        tab_b_scales = sbuf("tab_b_scales", [P, T // 4], I32)
        wb_scales_raw = sbuf("wb_scales_raw", [P, R // 4], I32)
        tab_a_words = sbuf("tab_a_words", [P, T], I32)
        tab_b_words = sbuf("tab_b_words", [P, T], I32)
        wb_words_raw = sbuf("wb_words_raw", [P, R // 2], I32)
        wa_rows = wa.rearrange("(p i) r -> p i r", i=PACK)
        en_rows = en.rearrange("(p t) n -> p t n", t=PACK)
        wa_raw = sbuf("wa_raw", [P, PACK, R], F32)
        en_raw = [sbuf("en_raw_%d" % h, [P, PACK, EN_CUTS[h + 1] - EN_CUTS[h]], F32) for h in range(2)]
        sync4 = (nc.sync, nc.sync, nc.sync, nc.sync)
        mixed4 = (nc.sync, nc.sync, nc.scalar, nc.scalar)
        made = {}

        def once(name, shape, dtype):
            if name not in made:
                made.update({name: sbuf(name, shape, dtype)})
            return made[name]

        def load_words(tile, words):
            nc.sync.dma_start(out=tile[:], in_=words[0].rearrange("p t i -> p (t i)").bitcast(I32))

        def load_wa(pair):
            nc.sync.dma_start(out=wa_raw[:, 2 * pair : 2 * pair + 2, :], in_=wa_rows[:, 2 * pair : 2 * pair + 2, :])

        def load_en(h):
            nc.sync.dma_start(out=en_raw[h][:], in_=en_rows[:, :, EN_CUTS[h] : EN_CUTS[h + 1]])

        def round_wa(engine, i0, i1, m0, m1):
            src = wa_raw[:, i0:i1, PACK * m0 : PACK * m1].rearrange("p i (m t) -> p m t i", t=PACK)
            dst = once("wa_bf", [P, PACK, P, PACK], BF16)[:, :, m0:m1, i0:i1].rearrange("p t m i -> p m t i")
            if engine == "scalar":
                nc.scalar.activation(out=dst, in_=src, func=ACT.Copy, scale=-1.0)
            else:
                nc.vector.tensor_scalar_mul(dst, src, -1.0)

        def deal_wb_words():
            nc.vector.tensor_copy(
                out=once("wb_codes", [P, 2 * R], U8)[:].bitcast(U16).rearrange("p (t m) -> p t m", t=PACK),
                in_=wb_words_raw[:].bitcast(U16).rearrange("p (m t) -> p t m", t=PACK),
            )

        def deal_wb_scales():
            nc.vector.tensor_copy(
                out=once("wb_plane", [P, R], U8)[:].rearrange("p (t m) -> p t m", t=PACK),
                in_=wb_scales_raw[:].bitcast(U8).rearrange("p (m t) -> p t m", t=PACK),
            )

        picked = {}

        def gather(kind, c0, c1):
            window, offsets, dtype = {
                "a_words": (tab_a_words, list_a, U32),
                "a_scales": (tab_a_scales, list_a, U8),
                "b_words": (tab_b_words, list_b, U32),
                "b_scales": (tab_b_scales, list_b, U8),
            }[kind]
            tile = sbuf("%s_%d" % (kind, c0), [P, JC * (c1 - c0)], dtype)
            nc.vector.tensor_copy(tile[:], window[:].bitcast(dtype).indirect(offsets[:, 8 * c0 : 8 * c1]))
            for c in range(c0, c1):
                picked.update({(kind, c): tile[(A_PLANE if kind == "a_scales" else 0) :, JC * (c - c0) : JC * (c - c0 + 1)]})

        diff = [psum.tile([P, PACK, JC], F32, name="bank") for c in range(CHUNKS)]

        def project_b(c):
            for t in range(PACK):
                nc.tensor.matmul_mx(
                    out=diff[c][:, t, :],
                    lhsT=made["wb_codes"][:, 2 * P * t : 2 * P * (t + 1)].bitcast(FP4X4),
                    lhsT_scale=made["wb_plane"][:, P * t : P * (t + 1)],
                    rhs=picked[("b_words", c)].bitcast(FP8X4),
                    rhs_scale=picked[("b_scales", c)],
                    start=(t == 0),
                    stop=False,
                )

        def quantize_wa(t0, t1):
            cols = slice(P * t0, P * t1)
            nc.vector.quantize_mx(
                out=once("wa_codes", [P, R], U32)[:, cols].bitcast(FP8X4),
                scales=once("wa_scales", [P, R], U8)[:, cols],
                in_=made["wa_bf"][:, t0:t1, :, :].rearrange("p t m i -> p (t m i)"),
            )

        def project_a(c):
            for t in range(PACK):
                cols = slice(P * t, P * (t + 1))
                nc.tensor.matmul_mx(
                    out=diff[c][:, t, :],
                    lhsT=made["wa_codes"][:, cols].bitcast(FP8X4),
                    lhsT_scale=made["wa_scales"][:, cols],
                    rhs=picked[("a_words", c)].bitcast(FP8X4),
                    rhs_scale=picked[("a_scales", c)],
                    start=False,
                    stop=(t == PACK - 1),
                )

        def h_chunk(c):
            if c == 0:
                return once("h_first", [P, JC, PACK], BF16)[:]
            return once("h_rest", [P, J - JC, PACK], BF16)[:, JC * (c - 1) : JC * c, :]

        def rectify(c):
            nc.scalar.activation(out=h_chunk(c), in_=diff[c][:].rearrange("p t j -> p j t"), func=ACT.Abs)

        def round_en(engine, half, n0, n1):
            dst = once("en_bf_%d" % half, [P, HALF, PACK], BF16)[:, n0:n1, :]
            src = en_raw[half][:, :, n0:n1]
            if engine == "gpsimd":
                nc.gpsimd.tensor_scalar(dst, src.rearrange("p t n -> p n t"), 1.0, 0.0, mybir.AluOpType.mult, mybir.AluOpType.add)
            elif engine == "scalar":
                nc.scalar.copy(out=dst.rearrange("p (c u) t -> p c t u", u=4), in_=src.rearrange("p t (c u) -> p c t u", u=4))
            else:
                nc.vector.tensor_copy(out=dst.rearrange("p (c u) t -> p c t u", u=4), in_=src.rearrange("p t (c u) -> p c t u", u=4))

        def quantize_h(c):
            js = slice(JC * c, JC * (c + 1))
            nc.vector.quantize_mx(
                out=once("h_codes", [P, J], U32)[:, js].bitcast(FP8X4),
                scales=once("h_scales", [P, J], U8)[:, js],
                in_=h_chunk(c).rearrange("p j t -> p (j t)"),
            )

        def quantize_en(half):
            nc.vector.quantize_mx(
                out=once("en_codes_%d" % half, [P, HALF], U32)[:].bitcast(FP8X4),
                scales=once("en_scales_%d" % half, [P, HALF], U8)[:],
                in_=made["en_bf_%d" % half][:].rearrange("p n t -> p (n t)"),
            )

        banks = {}

        def score(j0, width, m0, count, part=None):
            if (j0, m0) not in banks:
                banks.update({(j0, m0): (psum.tile([P, count, width], F32, name="bank"), width, count)})
            y = banks[(j0, m0)][0]
            a, b = (0, width) if part is None else (JC * part, JC * (part + 1))
            js = slice(j0 + a, j0 + b)
            for m in range(m0, m0 + count):
                ns = slice(P * (m % 2), P * (m % 2 + 1))
                nc.tensor.matmul_mx(
                    out=y[:, m - m0, a:b],
                    lhsT=made["en_codes_%d" % (m // 2)][:, ns].bitcast(FP8X4),
                    lhsT_scale=made["en_scales_%d" % (m // 2)][:, ns],
                    rhs=made["h_codes"][:, js].bitcast(FP8X4),
                    rhs_scale=made["h_scales"][:, js],
                    start=True,
                    stop=True,
                )

        def leave(j0, m0, engine, queue):
            y, width, count = banks[(j0, m0)]
            staged = sbuf("staged_%d_%d" % (j0, m0), [P, count, width], F32)
            if engine == "vector":
                nc.vector.tensor_copy(out=staged[:], in_=y[:])
            else:
                nc.scalar.copy(out=staged[:], in_=y[:])
            queue.dma_start(out=out[P * m0 : P * (m0 + count), j0 : j0 + width].rearrange("(m p) j -> p m j", p=P), in_=staged[:])

        nc.vector.memset(tab_b_scales[:], 0)
        nc.vector.memset(wb_scales_raw[:], 0)
        nc.vector.memset(tab_a_scales[:], 0)
        nc.sync.dma_start(out=wb_words_raw[:], in_=wb_words[0].bitcast(I32))
        nc.sync.dma_start(list_b[:], offs2)
        load_scale_rows(mixed4, tab_b_scales, tab2_scales)
        load_words(tab_b_words, tab2_words)
        load_wa(0)
        load_scale_rows(sync4, wb_scales_raw, wb_scales)
        load_wa(1)
        load_en(0)
        nc.sync.dma_start(list_a[:], offs)
        load_scale_rows(sync4, tab_a_scales, tab_scales, A_PLANE)
        load_words(tab_a_words, tab_words)
        load_en(1)
        round_wa("scalar", 0, 2, 0, WA_ON_SCALAR)
        round_wa("scalar", 2, 4, 0, WA_ON_SCALAR)
        deal_wb_words()
        gather("b_scales", 0, 4)
        gather("b_words", 0, 4)
        deal_wb_scales()
        project_b(0)
        project_b(1)
        project_b(2)
        project_b(3)
        round_wa("vector", 0, 4, WA_ON_SCALAR, P)
        quantize_wa(0, 4)
        gather("a_scales", 0, 2)
        round_en("scalar", 0, 0, HALF)
        round_en("gpsimd", 1, 0, EN_ON_GPSIMD)
        gather("a_words", 0, 1)
        gather("a_words", 1, 2)
        gather("a_words", 2, 3)
        gather("a_words", 3, 4)
        project_a(0)
        project_a(1)
        gather("a_scales", 2, 3)
        project_a(2)
        gather("a_scales", 3, 4)
        project_a(3)
        rectify(0)
        rectify(1)
        rectify(2)
        rectify(3)

        quantize_en(0)
        round_en("vector", 1, EN_ON_GPSIMD, HALF)
        quantize_h(0)
        quantize_en(1)
        quantize_h(1)
        score(0, 256, 0, 1)
        score(0, 256, 1, 1)
        score(0, 256, 2, 1)
        score(0, 256, 3, 1)
        leave(0, 0, "vector", nc.sync)
        quantize_h(2)
        for m in range(4):
            score(256, 256, m, 1, 0)
        quantize_h(3)
        for m in range(4):
            score(256, 256, m, 1, 1)
        leave(0, 1, "scalar", nc.scalar)
        leave(0, 2, "scalar", nc.scalar)
        leave(0, 3, "vector", nc.sync)
        leave(256, 0, "vector", nc.sync)
        leave(256, 1, "scalar", nc.scalar)
        leave(256, 2, "vector", nc.sync)
        leave(256, 3, "scalar", nc.scalar)
